import numpy as np
import ml_dtypes


def mxq(x, axis, fmt="e4m3"):
    dtype, down = {"e4m3": (ml_dtypes.float8_e4m3fn, 7), "e5m2": (ml_dtypes.float8_e5m2, 14)}[fmt]
    v = np.moveaxis(np.asarray(x, np.float32).astype(ml_dtypes.bfloat16).astype(np.float64), axis, -1)
    blocks = v.reshape(v.shape[:-1] + (-1, 32))
    amax = np.abs(blocks).max(-1, keepdims=True)
    byte = np.maximum(np.where(amax > 0, np.frexp(amax)[1] - 1 + 127, 0) - down, 1)
    scale = np.exp2(byte - 127.0)
    codes = (blocks / scale).astype(np.float32).astype(dtype).astype(np.float64)
    return np.moveaxis((codes * scale).reshape(v.shape), -1, axis)


WIDE = False


def mx_kscale(k):
    if not WIDE:
        return np.ones(k)
    levels = np.array([10, -10, 5, -5, 0])
    if k % 512:
        return np.exp2(np.random.permutation(np.resize(levels, k // 32))).repeat(32)
    a = np.empty((k // 512, 16))
    for p in range(k // 512):
        a[p, :8] = np.random.permutation(np.resize(levels, 8))
        for g in range(8):
            far = levels[np.abs(levels - a[p, g]) >= 10]
            a[p, g + 8] = far[np.random.randint(len(far))]
    return np.exp2(a.ravel()).repeat(32)


def f64(x):
    return np.asarray(x).astype(np.float64)


def striped(idx):
    return np.tile(idx.reshape(-1, 16).T, (8, 1)).astype(np.uint16)


def unstriped(offs):
    return offs[:16].T.reshape(-1).astype(np.int64)


def pack_weight(w):
    k, n = w.shape
    w = f64(np.asarray(w, np.float32).astype(ml_dtypes.bfloat16)).reshape(k // 32, 32, n)
    amax = np.abs(w).max(1)
    byte = np.clip(np.where(amax > 0, np.frexp(amax)[1] - 1 + 127 - 7, 1), 1, 254)
    scaled = (w * np.exp2(127.0 - byte)[:, None, :]).reshape(k, n).astype(np.float32)
    words = np.ascontiguousarray(scaled.reshape(k // 512, 128, 4, n).transpose(0, 1, 3, 2)).astype(ml_dtypes.float8_e4m3fn).view(np.uint8)
    return words, np.ascontiguousarray(byte.astype(np.uint8).reshape(k // 512, 16, n))


def unpack_weight(words, scales):
    g, p, n, _ = words.shape
    vals = np.ascontiguousarray(words).view(ml_dtypes.float8_e4m3fn).astype(np.float64) * np.repeat(np.exp2(scales.astype(np.float64) - 127.0), 8, axis=1)[..., None]
    return vals.transpose(0, 1, 3, 2).reshape(g * 512, n)


def relu2(v):
    return np.maximum(v, 0.0) ** 2


K, T, E, C, N = 1536, 1536, 8, 256, 128
PAD = 32


def by_expert(wq, xq):
    return np.concatenate([wq[e].T @ xq[:, e * C:(e + 1) * C] for e in range(E)], axis=1)


def setup_inputs():
    n = np.random.standard_normal
    s = mx_kscale(K)[:, None]
    first = np.random.permutation(np.repeat(np.arange(E), T // E))
    second = (first + 1 + np.random.permutation(np.repeat(np.arange(E - 1), -(-T // (E - 1)))[:T])) % E
    while np.bincount(second, minlength=E).max() != T // E:
        load = np.bincount(second, minlength=E); hi, lo = int(load.argmax()), int(load.argmin())
        t = np.flatnonzero((second == hi) & (first != lo))[0]; second[t] = lo
    slot_token = np.empty(E * C, np.int64); pos = np.empty((2, T), np.int64); fill = np.zeros(E, np.int64)
    place = np.stack([np.random.permutation(C) for _ in range(E)])
    for r, deal in enumerate((first, second)):
        for t in np.random.permutation(T):
            e = deal[t]
            if fill[e] < C: j = e * C + place[e, fill[e]]; fill[e] += 1; slot_token[j] = t; pos[r, t] = j
            else: pos[r, t] = E * C + t % PAD
    g = np.random.uniform(0.2, 0.8, T)
    packed = [pack_weight(m) for m in n((E, K, N)) / np.sqrt(K) / s[None]]
    return {
        "xT": (n((K, T)) * s).astype(np.float32),
        "w_words": np.stack([m[0] for m in packed]),
        "w_scales": np.stack([m[1] for m in packed]),
        "b": (0.3 * n((N, E))).astype(np.float32),
        "gate": np.stack([np.tile(g, (N, 1)), np.tile(1.0 - g, (N, 1))]).astype(np.float32),
        "offs": striped(slot_token),
        "pos1": striped(pos[0]),
        "pos2": striped(pos[1]),
    }


def reference(xT, w_words, w_scales, b, gate, offs, pos1, pos2):
    idx = unstriped(offs)
    w = np.stack([unpack_weight(w_words[e], w_scales[e]) for e in range(E)])
    xq = mxq(f64(xT)[:, idx], 0, "e4m3")
    y = by_expert(w, xq)
    y = relu2(y + np.repeat(f64(b), C, axis=1))
    y = np.concatenate([y, np.zeros((N, PAD))], axis=1)
    return f64(gate[0]) * y[:, unstriped(pos1)] + f64(gate[1]) * y[:, unstriped(pos2)]

@@ -1,0 +1,143 @@
+from contextlib import ExitStack
+
+import concourse.mybir as mybir
+
+K, T, E, C, N = 1536, 1536, 8, 256, 128
+S = E * C
+PAD = 32
+P = 128
+PACK = 4
+K_PASS = P * PACK
+PASSES = K // K_PASS
+
+FLOPS = 2 * K * N * S
+
+F32 = mybir.dt.float32
+BF16 = mybir.dt.bfloat16
+I32 = mybir.dt.int32
+U32 = mybir.dt.uint32
+U16 = mybir.dt.uint16
+U8 = mybir.dt.uint8
+FP8X4 = mybir.dt.float8_e4m3fn_x4
+ACT = mybir.ActivationFunctionType
+MULT = mybir.AluOpType.mult
+ADD = mybir.AluOpType.add
+
+LOADS = (
+    (0, 0, 512), (0, 512, 512), (0, 1024, 512),
+    (1, 0, 512), (1, 512, 512), (1, 1024, 512),
+    (2, 0, 512), (2, 512, 512), (2, 1024, 256), (2, 1280, 256),
+)
+VECTOR_SHARE = (4, 8, 8, 0, 0, 4, 0, 0, 0, 6)
+
+
+def tile_moe_cap2_lin_relu2_kernel(tc, xT, w_words, w_scales, b, gate, offs, pos1, pos2, out):
+    nc = tc.nc
+    with ExitStack() as ctx:
+        keep = ctx.enter_context(tc.tile_pool(name="keep", bufs=1))
+        psum = ctx.enter_context(tc.psum_pool(name="psum", bufs=1))
+
+        offs_sb = keep.tile([P, S // 16], U16, name="offs_sb")
+        pos1_sb = keep.tile([P, T // 16], U16, name="pos1_sb")
+        pos2_sb = keep.tile([P, T // 16], U16, name="pos2_sb")
+        codes = [keep.tile([P, T], U32, name=f"codes{a}", align_bytes=64) for a in range(PASSES)]
+        planes = keep.tile([P, T], U8, name="planes", align_bytes=64)
+        slot_codes = [keep.tile([P, S], U32, name=f"slot_codes{a}", align_bytes=64) for a in range(PASSES)]
+        slot_planes = keep.tile([P, S], U8, name="slot_planes", align_bytes=64)
+        w_sb = keep.tile([P, E * PASSES, N], U32, name="w_sb", align_bytes=64)
+        w_planes = keep.tile([P, E * N], U8, name="w_planes", align_bytes=64)
+        b_sb = keep.tile([P, E], F32, name="b_sb")
+        gate_sb = [keep.tile([P, T], F32, name=f"gate_sb{g}") for g in range(2)]
+        y = keep.tile([P, S + PAD], F32, name="y")
+        warm = keep.tile([P, 8], F32, name="warm")
+        warmed = keep.tile([P, 8], F32, name="warmed")
+        banks = [psum.tile([P, C], F32, name=f"bank{e}") for e in range(E)]
+
+        nc.vector.memset(warm[:], 0.0)
+        nc.scalar.activation(warmed[:], warm[:], ACT.Square)
+        nc.vector.memset(w_planes[:].bitcast(I32), 0)
+        nc.vector.memset(planes[:].bitcast(I32), 0)
+
+        raws = []
+        for i, (a, t0, width) in enumerate(LOADS):
+            raw = keep.tile([P, PACK, width], F32, name=f"raw{i}")
+            nc.sync.dma_start(out=raw[:], in_=xT[a * K_PASS : (a + 1) * K_PASS, t0 : t0 + width].rearrange("(p j) t -> p j t", j=PACK))
+            raws.append(raw)
+            if i == 1:
+                nc.sync.dma_start(offs_sb[:], offs)
+        nc.gpsimd.dma_start(out=b_sb[:], in_=b)
+        scale_rows = w_scales.rearrange("e a (q r) n -> a r q e n", r=4)
+        for a in range(PASSES):
+            for r in range(4):
+                nc.gpsimd.dma_start(
+                    out=w_planes[4 * a + r : P : 32, :].bitcast(I32).rearrange("q (e n) -> q e n", e=E),
+                    in_=scale_rows[a, r].bitcast(I32),
+                )
+        nc.gpsimd.memset(y[:, S : S + PAD], 0.0)
+        for e in range(0, E, 2):
+            nc.sync.dma_start(
+                out=w_sb[:, e * PASSES : (e + 2) * PASSES, :].bitcast(I32),
+                in_=w_words[e : e + 2].rearrange("e a p n r -> p (e a) (n r)").bitcast(I32),
+            )
+        nc.sync.dma_start(pos1_sb[:], pos1)
+        nc.sync.dma_start(pos2_sb[:], pos2)
+        for half in (slice(0, 768), slice(768, T)):
+            for g in range(2):
+                nc.sync.dma_start(out=gate_sb[g][:, half], in_=gate[g, :, half])
+
+        for i, (a, t0, width) in enumerate(LOADS):
+            for u0 in range(0, width, 512):
+                n = min(512, width - u0)
+                grouped = keep.tile([P, n, PACK], BF16, name=f"grouped{i}_{u0}", align_bytes=64)
+                cut = n - n * VECTOR_SHARE[i] // 128 * 8
+                for lo, hi, engine in ((0, cut, 0), (cut, n, 1)):
+                    if lo == hi:
+                        continue
+                    dst = grouped[:, lo:hi, :].rearrange("p (c i) j -> p c j i", i=4)
+                    source = raws[i][:, :, u0 + lo : u0 + hi].rearrange("p j (c i) -> p c j i", i=4)
+                    if engine == 0:
+                        nc.scalar.activation(dst, source, ACT.Copy)
+                    else:
+                        nc.vector.tensor_copy(dst, source)
+                cols = slice(t0 + u0, t0 + u0 + n)
+                nc.vector.quantize_mx(
+                    out=codes[a][:, cols].bitcast(FP8X4),
+                    scales=planes[4 * a : P, cols],
+                    in_=grouped[:].rearrange("p t j -> p (t j)"),
+                )
+
+        def gather(dst, window, lo, hi):
+            nc.vector.tensor_copy(dst[:, lo:hi], window[:].indirect(offs_sb[:, lo // 16 : hi // 16]))
+
+        for a in range(PASSES - 1):
+            for lo in range(0, S, 1024):
+                gather(slot_codes[a], codes[a], lo, lo + 1024)
+
+        for lo, hi in ((0, 512), (512, 1024), (1024, 1536), (1536, 1792), (1792, 2048)):
+            gather(slot_planes, planes, lo, hi)
+            gather(slot_codes[PASSES - 1], codes[PASSES - 1], lo, hi)
+            for e in range(lo // C, hi // C):
+                slots = slice(e * C, (e + 1) * C)
+                for a in range(PASSES):
+                    nc.tensor.matmul_mx(
+                        out=banks[e][:],
+                        lhsT=w_sb[:, e * PASSES + a, :].bitcast(FP8X4),
+                        lhsT_scale=w_planes[4 * a : P, e * N : (e + 1) * N],
+                        rhs=slot_codes[a][:, slots].bitcast(FP8X4),
+                        rhs_scale=slot_planes[4 * a : P, slots],
+                        start=(a == 0),
+                        stop=(a == PASSES - 1),
+                    )
+                relu = keep.tile([P, C], F32, name=f"relu{e}")
+                nc.scalar.activation(relu[:], banks[e][:], ACT.Relu, bias=b_sb[:, e : e + 1])
+                nc.scalar.activation(y[:, slots], relu[:], ACT.Square)
+
+        for i, (lo, hi) in enumerate(((0, 768), (768, 1280), (1280, 1536))):
+            picked = []
+            for g, pos_sb in enumerate((pos1_sb, pos2_sb)):
+                z = keep.tile([P, hi - lo], F32, name=f"z{g}_{i}")
+                nc.vector.tensor_tensor(z[:], y[:].indirect(pos_sb[:, lo // 16 : hi // 16]), gate_sb[g][:, lo:hi], MULT)
+                picked.append(z)
+            total = keep.tile([P, hi - lo], F32, name=f"total{i}")
+            nc.vector.tensor_tensor(total[:], picked[0][:], picked[1][:], ADD)
+            nc.sync.dma_start(out=out[:, lo:hi], in_=total[:])

@@ -45,7 +45,7 @@ def tile_moe_cap2_lin_relu2_kernel(tc, xT, w_words, w_scales, b, gate, offs, pos
         slot_codes = [keep.tile([P, S], U32, name=f"slot_codes{a}", align_bytes=64) for a in range(PASSES)]
         slot_planes = keep.tile([P, S], U8, name="slot_planes", align_bytes=64)
         w_sb = keep.tile([P, E * PASSES, N], U32, name="w_sb", align_bytes=64)
-        w_planes = keep.tile([P, E * N], U8, name="w_planes", align_bytes=64)
+        w_planes = keep.tile([P, E * PASSES, N], U8, name="w_planes", align_bytes=64)
         b_sb = keep.tile([P, E], F32, name="b_sb")
         gate_sb = [keep.tile([P, T], F32, name=f"gate_sb{g}") for g in range(2)]
         y = keep.tile([P, S + PAD], F32, name="y")
@@ -56,6 +56,7 @@ def tile_moe_cap2_lin_relu2_kernel(tc, xT, w_words, w_scales, b, gate, offs, pos
         nc.vector.memset(warm[:], 0.0)
         nc.scalar.activation(warmed[:], warm[:], ACT.Square)
         nc.vector.memset(w_planes[:].bitcast(I32), 0)
+        nc.vector.memset(y[:, S : S + PAD], 0.0)
         nc.vector.memset(planes[:].bitcast(I32), 0)
 
         raws = []
@@ -65,15 +66,10 @@ def tile_moe_cap2_lin_relu2_kernel(tc, xT, w_words, w_scales, b, gate, offs, pos
             raws.append(raw)
             if i == 1:
                 nc.sync.dma_start(offs_sb[:], offs)
-        nc.gpsimd.dma_start(out=b_sb[:], in_=b)
-        scale_rows = w_scales.rearrange("e a (q r) n -> a r q e n", r=4)
-        for a in range(PASSES):
-            for r in range(4):
-                nc.gpsimd.dma_start(
-                    out=w_planes[4 * a + r : P : 32, :].bitcast(I32).rearrange("q (e n) -> q e n", e=E),
-                    in_=scale_rows[a, r].bitcast(I32),
-                )
-        nc.gpsimd.memset(y[:, S : S + PAD], 0.0)
+        nc.sync.dma_start(out=b_sb[:], in_=b)
+        scale_rows = w_scales.rearrange("e a (q r) n -> r q (e a) n", r=4)
+        for r in range(4):
+            nc.sync.dma_start(out=w_planes[r:P:32].bitcast(I32), in_=scale_rows[r].bitcast(I32))
         for e in range(0, E, 2):
             nc.sync.dma_start(
                 out=w_sb[:, e * PASSES : (e + 2) * PASSES, :].bitcast(I32),
@@ -122,7 +118,7 @@ def tile_moe_cap2_lin_relu2_kernel(tc, xT, w_words, w_scales, b, gate, offs, pos
                     nc.tensor.matmul_mx(
                         out=banks[e][:],
                         lhsT=w_sb[:, e * PASSES + a, :].bitcast(FP8X4),
-                        lhsT_scale=w_planes[4 * a : P, e * N : (e + 1) * N],
+                        lhsT_scale=w_planes[:, e * PASSES + a, :],
                         rhs=slot_codes[a][:, slots].bitcast(FP8X4),
                         rhs_scale=slot_planes[4 * a : P, slots],
                         start=(a == 0),

@@ -1,6 +1,7 @@
 from contextlib import ExitStack
 
 import concourse.mybir as mybir
+from concourse.masks import make_identity
 
 K, T, E, C, N = 1536, 1536, 8, 256, 128
 S = E * C
@@ -22,6 +23,7 @@ FP8X4 = mybir.dt.float8_e4m3fn_x4
 ACT = mybir.ActivationFunctionType
 MULT = mybir.AluOpType.mult
 ADD = mybir.AluOpType.add
+MAX = mybir.AluOpType.max
 
 LOADS = (
     (0, 0, 512), (0, 512, 512), (0, 1024, 512),
@@ -51,7 +53,8 @@ def tile_moe_cap2_lin_relu2_kernel(tc, xT, w_words, w_scales, b, gate, offs, pos
         y = keep.tile([P, S + PAD], F32, name="y")
         warm = keep.tile([P, 8], F32, name="warm")
         warmed = keep.tile([P, 8], F32, name="warmed")
-        banks = [psum.tile([P, C], F32, name=f"bank{e}") for e in range(E)]
+        ident = keep.tile([P, P], F32, name="ident")
+        make_identity(nc, ident[:])
 
         nc.vector.memset(warm[:], 0.0)
         nc.scalar.activation(warmed[:], warm[:], ACT.Square)
@@ -112,11 +115,14 @@ def tile_moe_cap2_lin_relu2_kernel(tc, xT, w_words, w_scales, b, gate, offs, pos
         for lo, hi in ((0, 512), (512, 1024), (1024, 1536), (1536, 1792), (1792, 2048)):
             gather(slot_planes, planes, lo, hi)
             gather(slot_codes[PASSES - 1], codes[PASSES - 1], lo, hi)
-            for e in range(lo // C, hi // C):
-                slots = slice(e * C, (e + 1) * C)
-                for a in range(PASSES):
+            groups = [(e * C, C) for e in range(lo // C, hi // C)] if hi < S else [(lo, P), (lo + P, P)]
+            sums = [psum.tile([P, width], F32, name="acc", bufs=4) for first, width in groups]
+            for a in range(PASSES):
+                for (first, width), acc in zip(groups, sums):
+                    e = first // C
+                    slots = slice(first, first + width)
                     nc.tensor.matmul_mx(
-                        out=banks[e][:],
+                        out=acc[:],
                         lhsT=w_sb[:, e * PASSES + a, :].bitcast(FP8X4),
                         lhsT_scale=w_planes[:, e * PASSES + a, :],
                         rhs=slot_codes[a][:, slots].bitcast(FP8X4),
@@ -124,16 +130,50 @@ def tile_moe_cap2_lin_relu2_kernel(tc, xT, w_words, w_scales, b, gate, offs, pos
                         start=(a == 0),
                         stop=(a == PASSES - 1),
                     )
-                relu = keep.tile([P, C], F32, name=f"relu{e}")
-                nc.scalar.activation(relu[:], banks[e][:], ACT.Relu, bias=b_sb[:, e : e + 1])
-                nc.scalar.activation(y[:, slots], relu[:], ACT.Square)
+            for (first, width), acc in zip(groups, sums):
+                e = first // C
+                relu = keep.tile([P, width], F32, name=f"relu{first}")
+                if hi < S:
+                    nc.scalar.activation(relu[:], acc[:], ACT.Relu, bias=b_sb[:, e : e + 1])
+                else:
+                    nc.vector.tensor_scalar(relu[:], acc[:], b_sb[:, e : e + 1], 0.0, ADD, MAX)
+                nc.scalar.activation(y[:, first : first + width], relu[:], ACT.Square)
 
-        for i, (lo, hi) in enumerate(((0, 768), (768, 1280), (1280, 1536))):
-            picked = []
-            for g, pos_sb in enumerate((pos1_sb, pos2_sb)):
-                z = keep.tile([P, hi - lo], F32, name=f"z{g}_{i}")
-                nc.vector.tensor_tensor(z[:], y[:].indirect(pos_sb[:, lo // 16 : hi // 16]), gate_sb[g][:, lo:hi], MULT)
-                picked.append(z)
-            total = keep.tile([P, hi - lo], F32, name=f"total{i}")
-            nc.vector.tensor_tensor(total[:], picked[0][:], picked[1][:], ADD)
+        def fetch(g, lo, hi):
+            z = keep.tile([P, hi - lo], F32, name=f"z{g}_{lo}")
+            pos_sb = (pos1_sb, pos2_sb)[g]
+            nc.vector.tensor_tensor(z[:], y[:].indirect(pos_sb[:, lo // 16 : hi // 16]), gate_sb[g][:, lo:hi], MULT)
+            return z
+
+        def turn_and_add(lo, hi):
+            first, second = fetch(0, lo, hi), fetch(1, lo, hi)
+            turned = psum.tile([P, hi - lo], F32, name="turned", bufs=2)
+            for c in range(0, hi - lo, P):
+                for g, z in enumerate((first, second)):
+                    nc.tensor.matmul(turned[:, c : c + P], z[:, c : c + P], ident[:], start=(g == 0), stop=(g == 1), is_transpose=True)
+            by_token = keep.tile([P, hi - lo], F32, name=f"by_token{lo}")
+            nc.scalar.activation(by_token[:], turned[:], ACT.Copy)
+            return by_token
+
+        def turn_back(by_token, lo, hi):
+            back = psum.tile([P, hi - lo], F32, name="back", bufs=2)
+            for c in range(0, hi - lo, P):
+                nc.tensor.transpose(back[:, c : c + P], by_token[:, c : c + P], ident[:])
+            total = keep.tile([P, hi - lo], F32, name=f"total{lo}")
+            nc.scalar.activation(total[:], back[:], ACT.Copy)
+            nc.scalar.dma_start(out=out[:, lo:hi], in_=total[:])
+
+        def add_on_vector(first, second, lo, hi):
+            total = keep.tile([P, hi - lo], F32, name=f"total{lo}")
+            nc.vector.tensor_tensor(total[:], first[:], second[:], ADD)
             nc.sync.dma_start(out=out[:, lo:hi], in_=total[:])
+
+        waiting = None
+        for lo in range(0, 768, 256):
+            summed = (turn_and_add(lo, lo + 256), lo, lo + 256)
+            if waiting:
+                turn_back(*waiting)
+            waiting = summed
+        turn_back(*waiting)
+        for lo, hi in ((768, 1152), (1152, 1408), (1408, T)):
+            add_on_vector(fetch(0, lo, hi), fetch(1, lo, hi), lo, hi)

@@ -25,12 +25,13 @@ MULT = mybir.AluOpType.mult
 ADD = mybir.AluOpType.add
 MAX = mybir.AluOpType.max
 
-LOADS = (
-    (0, 0, 512), (0, 512, 512), (0, 1024, 512),
-    (1, 0, 512), (1, 512, 512), (1, 1024, 512),
-    (2, 0, 512), (2, 512, 512), (2, 1024, 256), (2, 1280, 256),
-)
-VECTOR_SHARE = (4, 8, 8, 0, 0, 4, 0, 0, 0, 6)
+LOADS = ((512, 512, 256, 128, 128), (256,) * 6, (256,) * 6)
+SHARES = ((256, 256, 128, 64, 64), (0, 0, 0, 0, 0, 128), (0, 0, 0, 0, 0, 128))
+UNITS = ((256, 256, 256, 256, 256, 128, 128), (512, 512, 256, 128, 128), (512, 512, 256, 128, 128))
+
+
+def spans(widths):
+    return [(sum(widths[:i]), sum(widths[: i + 1])) for i in range(len(widths))]
 
 
 def tile_moe_cap2_lin_relu2_kernel(tc, xT, w_words, w_scales, b, gate, offs, pos1, pos2, out):
@@ -62,12 +63,13 @@ def tile_moe_cap2_lin_relu2_kernel(tc, xT, w_words, w_scales, b, gate, offs, pos
         nc.vector.memset(y[:, S : S + PAD], 0.0)
         nc.vector.memset(planes[:].bitcast(I32), 0)
 
-        raws = []
-        for i, (a, t0, width) in enumerate(LOADS):
-            raw = keep.tile([P, PACK, width], F32, name=f"raw{i}")
-            nc.sync.dma_start(out=raw[:], in_=xT[a * K_PASS : (a + 1) * K_PASS, t0 : t0 + width].rearrange("(p j) t -> p j t", j=PACK))
-            raws.append(raw)
-            if i == 1:
+        raws = {}
+        for a in range(PASSES):
+            for lo, hi in spans(LOADS[a]):
+                raw = keep.tile([P, PACK, hi - lo], F32, name=f"raw{a}_{lo}")
+                nc.sync.dma_start(out=raw[:], in_=xT[a * K_PASS : (a + 1) * K_PASS, lo:hi].rearrange("(p j) t -> p j t", j=PACK))
+                raws[a, lo] = raw
+            if a == 0:
                 nc.sync.dma_start(offs_sb[:], offs)
         nc.sync.dma_start(out=b_sb[:], in_=b)
         scale_rows = w_scales.rearrange("e a (q r) n -> r q (e a) n", r=4)
@@ -84,24 +86,23 @@ def tile_moe_cap2_lin_relu2_kernel(tc, xT, w_words, w_scales, b, gate, offs, pos
             for g in range(2):
                 nc.sync.dma_start(out=gate_sb[g][:, half], in_=gate[g, :, half])
 
-        for i, (a, t0, width) in enumerate(LOADS):
-            for u0 in range(0, width, 512):
-                n = min(512, width - u0)
-                grouped = keep.tile([P, n, PACK], BF16, name=f"grouped{i}_{u0}", align_bytes=64)
-                cut = n - n * VECTOR_SHARE[i] // 128 * 8
-                for lo, hi, engine in ((0, cut, 0), (cut, n, 1)):
-                    if lo == hi:
-                        continue
-                    dst = grouped[:, lo:hi, :].rearrange("p (c i) j -> p c j i", i=4)
-                    source = raws[i][:, :, u0 + lo : u0 + hi].rearrange("p j (c i) -> p c j i", i=4)
-                    if engine == 0:
-                        nc.scalar.activation(dst, source, ACT.Copy)
-                    else:
-                        nc.vector.tensor_copy(dst, source)
-                cols = slice(t0 + u0, t0 + u0 + n)
+        for a in range(PASSES):
+            for u0, u1 in spans(UNITS[a]):
+                grouped = keep.tile([P, u1 - u0, PACK], BF16, name=f"grouped{a}_{u0}", align_bytes=64)
+                for (l0, l1), share in zip(spans(LOADS[a]), SHARES[a]):
+                    for lo, hi, on_vector in ((l0, l1 - share, False), (l1 - share, l1, True)):
+                        lo, hi = max(lo, u0), min(hi, u1)
+                        if lo >= hi:
+                            continue
+                        dst = grouped[:, lo - u0 : hi - u0, :].rearrange("p (c i) j -> p c j i", i=4)
+                        source = raws[a, l0][:, :, lo - l0 : hi - l0].rearrange("p j (c i) -> p c j i", i=4)
+                        if on_vector:
+                            nc.vector.tensor_copy(dst, source)
+                        else:
+                            nc.scalar.activation(dst, source, ACT.Copy)
                 nc.vector.quantize_mx(
-                    out=codes[a][:, cols].bitcast(FP8X4),
-                    scales=planes[4 * a : P, cols],
+                    out=codes[a][:, u0:u1].bitcast(FP8X4),
+                    scales=planes[4 * a : P, u0:u1],
                     in_=grouped[:].rearrange("p t j -> p (t j)"),
                 )
 
@@ -112,8 +113,9 @@ def tile_moe_cap2_lin_relu2_kernel(tc, xT, w_words, w_scales, b, gate, offs, pos
             for lo in range(0, S, 1024):
                 gather(slot_codes[a], codes[a], lo, lo + 1024)
 
-        for lo, hi in ((0, 512), (512, 1024), (1024, 1536), (1536, 1792), (1792, 2048)):
-            gather(slot_planes, planes, lo, hi)
+        for lo, hi in ((0, 512), (512, 1024), (1024, 1280), (1280, 1536), (1536, 1792), (1792, 2048)):
+            if lo % 1024 == 0:
+                gather(slot_planes, planes, lo, lo + 1024)
             gather(slot_codes[PASSES - 1], codes[PASSES - 1], lo, hi)
             groups = [(e * C, C) for e in range(lo // C, hi // C)] if hi < S else [(lo, P), (lo + P, P)]
             sums = [psum.tile([P, width], F32, name="acc", bufs=4) for first, width in groups]
@@ -169,11 +171,11 @@ def tile_moe_cap2_lin_relu2_kernel(tc, xT, w_words, w_scales, b, gate, offs, pos
             nc.sync.dma_start(out=out[:, lo:hi], in_=total[:])
 
         waiting = None
-        for lo in range(0, 768, 256):
-            summed = (turn_and_add(lo, lo + 256), lo, lo + 256)
+        for lo, hi in ((0, 512), (512, 768)):
+            summed = (turn_and_add(lo, hi), lo, hi)
             if waiting:
                 turn_back(*waiting)
             waiting = summed
         turn_back(*waiting)
-        for lo, hi in ((768, 1152), (1152, 1408), (1408, T)):
+        for lo, hi in ((768, 1280), (1280, 1408), (1408, T)):
             add_on_vector(fetch(0, lo, hi), fetch(1, lo, hi), lo, hi)

@@ -25,9 +25,9 @@ MULT = mybir.AluOpType.mult
 ADD = mybir.AluOpType.add
 MAX = mybir.AluOpType.max
 
-LOADS = ((512, 512, 256, 128, 128), (256,) * 6, (256,) * 6)
-SHARES = ((256, 256, 128, 64, 64), (0, 0, 0, 0, 0, 128), (0, 0, 0, 0, 0, 128))
-UNITS = ((256, 256, 256, 256, 256, 128, 128), (512, 512, 256, 128, 128), (512, 512, 256, 128, 128))
+LOADS = ((1024, 512), (512, 512, 512), (512, 512, 512))
+SHARES = ((512, 256), (0, 0, 256), (0, 0, 256))
+UNITS = ((256, 256, 512, 256, 256), (512, 512, 256, 256), (512, 512, 256, 256))
 
 
 def spans(widths):

@@ -26,8 +26,8 @@ ADD = mybir.AluOpType.add
 MAX = mybir.AluOpType.max
 
 LOADS = ((1024, 512), (512, 512, 512), (512, 512, 512))
-SHARES = ((512, 256), (0, 0, 256), (0, 0, 256))
-UNITS = ((256, 256, 512, 256, 256), (512, 512, 256, 256), (512, 512, 256, 256))
+SHARES = ((512, 128), (0, 0, 128), (0, 0, 128))
+UNITS = ((256, 256, 512, 256, 128, 128), (512, 512, 256, 128, 128), (512, 512, 256, 128, 128))
 
 
 def spans(widths):
@@ -82,7 +82,7 @@ def tile_moe_cap2_lin_relu2_kernel(tc, xT, w_words, w_scales, b, gate, offs, pos
             )
         nc.sync.dma_start(pos1_sb[:], pos1)
         nc.sync.dma_start(pos2_sb[:], pos2)
-        for half in (slice(0, 768), slice(768, T)):
+        for half in (slice(0, 640), slice(640, T)):
             for g in range(2):
                 nc.sync.dma_start(out=gate_sb[g][:, half], in_=gate[g, :, half])
 
@@ -113,9 +113,8 @@ def tile_moe_cap2_lin_relu2_kernel(tc, xT, w_words, w_scales, b, gate, offs, pos
             for lo in range(0, S, 1024):
                 gather(slot_codes[a], codes[a], lo, lo + 1024)
 
-        for lo, hi in ((0, 512), (512, 1024), (1024, 1280), (1280, 1536), (1536, 1792), (1792, 2048)):
-            if lo % 1024 == 0:
-                gather(slot_planes, planes, lo, lo + 1024)
+        for lo, hi in ((0, 512), (512, 1024), (1024, 1536), (1536, 1792), (1792, 2048)):
+            gather(slot_planes, planes, lo, hi)
             gather(slot_codes[PASSES - 1], codes[PASSES - 1], lo, hi)
             groups = [(e * C, C) for e in range(lo // C, hi // C)] if hi < S else [(lo, P), (lo + P, P)]
             sums = [psum.tile([P, width], F32, name="acc", bufs=4) for first, width in groups]
@@ -147,12 +146,11 @@ def tile_moe_cap2_lin_relu2_kernel(tc, xT, w_words, w_scales, b, gate, offs, pos
             nc.vector.tensor_tensor(z[:], y[:].indirect(pos_sb[:, lo // 16 : hi // 16]), gate_sb[g][:, lo:hi], MULT)
             return z
 
-        def turn_and_add(lo, hi):
-            first, second = fetch(0, lo, hi), fetch(1, lo, hi)
+        def turn_and_add(first, second, lo, hi):
             turned = psum.tile([P, hi - lo], F32, name="turned", bufs=2)
             for c in range(0, hi - lo, P):
                 for g, z in enumerate((first, second)):
-                    nc.tensor.matmul(turned[:, c : c + P], z[:, c : c + P], ident[:], start=(g == 0), stop=(g == 1), is_transpose=True)
+                    nc.tensor.matmul(turned[:, c : c + P], z[:, lo + c : lo + c + P], ident[:], start=(g == 0), stop=(g == 1), is_transpose=True)
             by_token = keep.tile([P, hi - lo], F32, name=f"by_token{lo}")
             nc.scalar.activation(by_token[:], turned[:], ACT.Copy)
             return by_token
@@ -171,11 +169,12 @@ def tile_moe_cap2_lin_relu2_kernel(tc, xT, w_words, w_scales, b, gate, offs, pos
             nc.sync.dma_start(out=out[:, lo:hi], in_=total[:])
 
         waiting = None
-        for lo, hi in ((0, 512), (512, 768)):
-            summed = (turn_and_add(lo, hi), lo, hi)
+        first, second = fetch(0, 0, 640), fetch(1, 0, 640)
+        for lo, hi in ((0, 256), (256, 512), (512, 640)):
+            summed = (turn_and_add(first, second, lo, hi), lo, hi)
             if waiting:
                 turn_back(*waiting)
             waiting = summed
         turn_back(*waiting)
-        for lo, hi in ((768, 1280), (1280, 1408), (1408, T)):
+        for lo, hi in ((640, 1152), (1152, 1408), (1408, T)):
             add_on_vector(fetch(0, lo, hi), fetch(1, lo, hi), lo, hi)

@@ -10,6 +10,7 @@ P = 128
 PACK = 4
 K_PASS = P * PACK
 PASSES = K // K_PASS
+WIDE = 2 * S
 
 FLOPS = 2 * K * N * S
 
@@ -43,8 +44,9 @@ def tile_moe_cap2_lin_relu2_kernel(tc, xT, w_words, w_scales, b, gate, offs, pos
         offs_sb = keep.tile([P, S // 16], U16, name="offs_sb")
         pos1_sb = keep.tile([P, T // 16], U16, name="pos1_sb")
         pos2_sb = keep.tile([P, T // 16], U16, name="pos2_sb")
-        codes = [keep.tile([P, T], U32, name=f"codes{a}", align_bytes=64) for a in range(PASSES)]
-        planes = keep.tile([P, T], U8, name="planes", align_bytes=64)
+        all_codes = keep.tile([P, (PASSES - 1) * T + WIDE], U32, name="all_codes", align_bytes=64)
+        codes = [all_codes[:, (PASSES - 1 - a) * T :] for a in range(PASSES)]
+        planes = keep.tile([P, S], U8, name="planes", align_bytes=64)
         slot_codes = [keep.tile([P, S], U32, name=f"slot_codes{a}", align_bytes=64) for a in range(PASSES)]
         slot_planes = keep.tile([P, S], U8, name="slot_planes", align_bytes=64)
         w_sb = keep.tile([P, E * PASSES, N], U32, name="w_sb", align_bytes=64)
@@ -62,6 +64,7 @@ def tile_moe_cap2_lin_relu2_kernel(tc, xT, w_words, w_scales, b, gate, offs, pos
         nc.vector.memset(w_planes[:].bitcast(I32), 0)
         nc.vector.memset(y[:, S : S + PAD], 0.0)
         nc.vector.memset(planes[:].bitcast(I32), 0)
+        nc.vector.memset(all_codes[:, PASSES * T :].bitcast(I32), 0)
 
         raws = {}
         for a in range(PASSES):
@@ -107,38 +110,51 @@ def tile_moe_cap2_lin_relu2_kernel(tc, xT, w_words, w_scales, b, gate, offs, pos
                 )
 
         def gather(dst, window, lo, hi):
-            nc.vector.tensor_copy(dst[:, lo:hi], window[:].indirect(offs_sb[:, lo // 16 : hi // 16]))
+            nc.vector.tensor_copy(dst[:, lo:hi], window.indirect(offs_sb[:, lo // 16 : hi // 16]))
 
         for a in range(PASSES - 1):
-            for lo in range(0, S, 1024):
-                gather(slot_codes[a], codes[a], lo, lo + 1024)
+            gather(slot_codes[a], codes[a][:, :WIDE], 0, S)
 
-        for lo, hi in ((0, 512), (512, 1024), (1024, 1536), (1536, 1792), (1792, 2048)):
-            gather(slot_planes, planes, lo, hi)
-            gather(slot_codes[PASSES - 1], codes[PASSES - 1], lo, hi)
-            groups = [(e * C, C) for e in range(lo // C, hi // C)] if hi < S else [(lo, P), (lo + P, P)]
-            sums = [psum.tile([P, width], F32, name="acc", bufs=4) for first, width in groups]
-            for a in range(PASSES):
-                for (first, width), acc in zip(groups, sums):
-                    e = first // C
-                    slots = slice(first, first + width)
-                    nc.tensor.matmul_mx(
-                        out=acc[:],
-                        lhsT=w_sb[:, e * PASSES + a, :].bitcast(FP8X4),
-                        lhsT_scale=w_planes[:, e * PASSES + a, :],
-                        rhs=slot_codes[a][:, slots].bitcast(FP8X4),
-                        rhs_scale=slot_planes[4 * a : P, slots],
-                        start=(a == 0),
-                        stop=(a == PASSES - 1),
-                    )
+        def multiply(acc, first, width, a):
+            e = first // C
+            slots = slice(first, first + width)
+            nc.tensor.matmul_mx(
+                out=acc[:],
+                lhsT=w_sb[:, e * PASSES + a, :].bitcast(FP8X4),
+                lhsT_scale=w_planes[:, e * PASSES + a, :],
+                rhs=slot_codes[a][:, slots].bitcast(FP8X4),
+                rhs_scale=slot_planes[4 * a : P, slots],
+                start=(a == 0),
+                stop=(a == PASSES - 1),
+            )
+
+        all_groups = [(e * C, C) for e in range(E - 1)] + [(S - C, P), (S - P, P)]
+        banks = {}
+        for lo, hi in ((0, 768), (768, 1536), (1536, 1792), (1792, 2048)):
+            if lo % T == 0:
+                gather(slot_planes, planes[:], lo, min(lo + T, S))
+                for first, width in all_groups:
+                    if lo <= first < lo + T:
+                        banks[first] = psum.tile([P, width], F32, name="bank", bufs=8)
+                        for a in range(PASSES - 1):
+                            multiply(banks[first], first, width, a)
+            gather(slot_codes[PASSES - 1], codes[PASSES - 1][:, :T], lo, hi)
+            groups = [(first, width) for first, width in all_groups if lo <= first < hi]
+            sums = [banks[first] for first, width in groups]
             for (first, width), acc in zip(groups, sums):
+                multiply(acc, first, width, PASSES - 1)
+            relus = [keep.tile([P, width], F32, name=f"relu{first}") for first, width in groups]
+            for (first, width), acc, relu in zip(groups, sums, relus):
                 e = first // C
-                relu = keep.tile([P, width], F32, name=f"relu{first}")
                 if hi < S:
                     nc.scalar.activation(relu[:], acc[:], ACT.Relu, bias=b_sb[:, e : e + 1])
                 else:
                     nc.vector.tensor_scalar(relu[:], acc[:], b_sb[:, e : e + 1], 0.0, ADD, MAX)
-                nc.scalar.activation(y[:, first : first + width], relu[:], ACT.Square)
+            for (first, width), relu in zip(groups, relus):
+                if hi < S:
+                    nc.scalar.activation(y[:, first : first + width], relu[:], ACT.Square)
+                else:
+                    nc.vector.tensor_tensor(y[:, first : first + width], relu[:], relu[:], MULT)
 
         def fetch(g, lo, hi):
             z = keep.tile([P, hi - lo], F32, name=f"z{g}_{lo}")
@@ -147,7 +163,7 @@ def tile_moe_cap2_lin_relu2_kernel(tc, xT, w_words, w_scales, b, gate, offs, pos
             return z
 
         def turn_and_add(first, second, lo, hi):
-            turned = psum.tile([P, hi - lo], F32, name="turned", bufs=2)
+            turned = psum.tile([P, hi - lo], F32, name="bank", bufs=8)
             for c in range(0, hi - lo, P):
                 for g, z in enumerate((first, second)):
                     nc.tensor.matmul(turned[:, c : c + P], z[:, lo + c : lo + c + P], ident[:], start=(g == 0), stop=(g == 1), is_transpose=True)
@@ -156,7 +172,7 @@ def tile_moe_cap2_lin_relu2_kernel(tc, xT, w_words, w_scales, b, gate, offs, pos
             return by_token
 
         def turn_back(by_token, lo, hi):
-            back = psum.tile([P, hi - lo], F32, name="back", bufs=2)
+            back = psum.tile([P, hi - lo], F32, name="bank", bufs=8)
             for c in range(0, hi - lo, P):
                 nc.tensor.transpose(back[:, c : c + P], by_token[:, c : c + P], ident[:])
             total = keep.tile([P, hi - lo], F32, name=f"total{lo}")

@@ -27,8 +27,8 @@ ADD = mybir.AluOpType.add
 MAX = mybir.AluOpType.max
 
 LOADS = ((1024, 512), (512, 512, 512), (512, 512, 512))
-SHARES = ((512, 128), (0, 0, 128), (0, 0, 128))
-UNITS = ((256, 256, 512, 256, 128, 128), (512, 512, 256, 128, 128), (512, 512, 256, 128, 128))
+SHARES = ((512, 256), (0, 0, 256), (0, 0, 256))
+UNITS = ((256, 256, 512, 128, 128, 256), (512, 512, 128, 128, 256), (512, 512, 128, 128, 256))
 
 
 def spans(widths):
@@ -146,12 +146,12 @@ def tile_moe_cap2_lin_relu2_kernel(tc, xT, w_words, w_scales, b, gate, offs, pos
             relus = [keep.tile([P, width], F32, name=f"relu{first}") for first, width in groups]
             for (first, width), acc, relu in zip(groups, sums, relus):
                 e = first // C
-                if hi < S:
+                if first < S - P:
                     nc.scalar.activation(relu[:], acc[:], ACT.Relu, bias=b_sb[:, e : e + 1])
                 else:
                     nc.vector.tensor_scalar(relu[:], acc[:], b_sb[:, e : e + 1], 0.0, ADD, MAX)
             for (first, width), relu in zip(groups, relus):
-                if hi < S:
+                if first < S - P:
                     nc.scalar.activation(y[:, first : first + width], relu[:], ACT.Square)
                 else:
                     nc.vector.tensor_tensor(y[:, first : first + width], relu[:], relu[:], MULT)

@@ -54,15 +54,13 @@ def tile_moe_cap2_lin_relu2_kernel(tc, xT, w_words, w_scales, b, gate, offs, pos
         b_sb = keep.tile([P, E], F32, name="b_sb")
         gate_sb = [keep.tile([P, T], F32, name=f"gate_sb{g}") for g in range(2)]
         y = keep.tile([P, S + PAD], F32, name="y")
-        warm = keep.tile([P, 8], F32, name="warm")
-        warmed = keep.tile([P, 8], F32, name="warmed")
+        zeros = keep.tile([P, PAD], F32, name="zeros")
         ident = keep.tile([P, P], F32, name="ident")
         make_identity(nc, ident[:])
 
-        nc.vector.memset(warm[:], 0.0)
-        nc.scalar.activation(warmed[:], warm[:], ACT.Square)
+        nc.vector.memset(zeros[:], 0.0)
+        nc.scalar.activation(y[:, S : S + PAD], zeros[:], ACT.Square)
         nc.vector.memset(w_planes[:].bitcast(I32), 0)
-        nc.vector.memset(y[:, S : S + PAD], 0.0)
         nc.vector.memset(planes[:].bitcast(I32), 0)
         nc.vector.memset(all_codes[:, PASSES * T :].bitcast(I32), 0)
 

@@ -31,6 +31,10 @@ SHARES = ((512, 256), (0, 0, 256), (0, 0, 256))
 UNITS = ((256, 256, 512, 128, 128, 256), (512, 512, 128, 128, 256), (512, 512, 128, 128, 256))
 
 
+PIECES = (256, 256, 256, 256, 256)
+TURNED = sum(PIECES)
+
+
 def spans(widths):
     return [(sum(widths[:i]), sum(widths[: i + 1])) for i in range(len(widths))]
 
@@ -52,7 +56,10 @@ def tile_moe_cap2_lin_relu2_kernel(tc, xT, w_words, w_scales, b, gate, offs, pos
         w_sb = keep.tile([P, E * PASSES, N], U32, name="w_sb", align_bytes=64)
         w_planes = keep.tile([P, E * PASSES, N], U8, name="w_planes", align_bytes=64)
         b_sb = keep.tile([P, E], F32, name="b_sb")
-        gate_sb = [keep.tile([P, T], F32, name=f"gate_sb{g}") for g in range(2)]
+        first_col = (0, TURNED)
+        gate_sb = [keep.tile([P, T - first_col[g]], F32, name=f"gate_sb{g}") for g in range(2)]
+        gate_rows = keep.tile([P, P], F32, name="gate_rows")
+        gate_cols = keep.tile([P, TURNED // P], F32, name="gate_cols")
         y = keep.tile([P, S + PAD], F32, name="y")
         zeros = keep.tile([P, PAD], F32, name="zeros")
         ident = keep.tile([P, P], F32, name="ident")
@@ -60,6 +67,7 @@ def tile_moe_cap2_lin_relu2_kernel(tc, xT, w_words, w_scales, b, gate, offs, pos
 
         nc.vector.memset(zeros[:], 0.0)
         nc.scalar.activation(y[:, S : S + PAD], zeros[:], ACT.Square)
+        nc.vector.memset(gate_rows[:], 0.0)
         nc.vector.memset(w_planes[:].bitcast(I32), 0)
         nc.vector.memset(planes[:].bitcast(I32), 0)
         nc.vector.memset(all_codes[:, PASSES * T :].bitcast(I32), 0)
@@ -83,9 +91,9 @@ def tile_moe_cap2_lin_relu2_kernel(tc, xT, w_words, w_scales, b, gate, offs, pos
             )
         nc.sync.dma_start(pos1_sb[:], pos1)
         nc.sync.dma_start(pos2_sb[:], pos2)
-        for half in (slice(0, 640), slice(640, T)):
-            for g in range(2):
-                nc.sync.dma_start(out=gate_sb[g][:, half], in_=gate[g, :, half])
+        nc.sync.dma_start(out=gate_rows[: TURNED // P, :], in_=gate[1, 0, :TURNED].rearrange("(c t) -> c t", t=P))
+        for g in range(2):
+            nc.sync.dma_start(out=gate_sb[g][:], in_=gate[g, :, first_col[g] :])
 
         for a in range(PASSES):
             for u0, u1 in spans(UNITS[a]):
@@ -112,6 +120,10 @@ def tile_moe_cap2_lin_relu2_kernel(tc, xT, w_words, w_scales, b, gate, offs, pos
 
         for a in range(PASSES - 1):
             gather(slot_codes[a], codes[a][:, :WIDE], 0, S)
+
+        gate_bank = psum.tile([P, P], F32, name="bank", bufs=8)
+        nc.tensor.transpose(gate_bank[:], gate_rows[:], ident[:])
+        nc.scalar.activation(gate_cols[:], gate_bank[:, : TURNED // P], ACT.Copy)
 
         def multiply(acc, first, width, a):
             e = first // C
@@ -157,38 +169,40 @@ def tile_moe_cap2_lin_relu2_kernel(tc, xT, w_words, w_scales, b, gate, offs, pos
         def fetch(g, lo, hi):
             z = keep.tile([P, hi - lo], F32, name=f"z{g}_{lo}")
             pos_sb = (pos1_sb, pos2_sb)[g]
-            nc.vector.tensor_tensor(z[:], y[:].indirect(pos_sb[:, lo // 16 : hi // 16]), gate_sb[g][:, lo:hi], MULT)
+            nc.vector.tensor_tensor(z[:], y[:].indirect(pos_sb[:, lo // 16 : hi // 16]), gate_sb[g][:, lo - first_col[g] : hi - first_col[g]], MULT)
             return z
 
-        def turn_and_add(first, second, lo, hi):
+        def fetch_and_turn(lo, hi):
+            plain = keep.tile([P, hi - lo], F32, name=f"plain{lo}")
+            nc.scalar.activation(plain[:], y[:].indirect(pos2_sb[:, lo // 16 : hi // 16]), ACT.Copy)
             turned = psum.tile([P, hi - lo], F32, name="bank", bufs=8)
             for c in range(0, hi - lo, P):
-                for g, z in enumerate((first, second)):
-                    nc.tensor.matmul(turned[:, c : c + P], z[:, lo + c : lo + c + P], ident[:], start=(g == 0), stop=(g == 1), is_transpose=True)
-            by_token = keep.tile([P, hi - lo], F32, name=f"by_token{lo}")
-            nc.scalar.activation(by_token[:], turned[:], ACT.Copy)
-            return by_token
+                nc.tensor.transpose(turned[:, c : c + P], plain[:, c : c + P], ident[:])
+            return turned
 
-        def turn_back(by_token, lo, hi):
+        def weigh_and_turn_back(turned, lo, hi):
+            by_token = keep.tile([P, hi - lo], F32, name=f"by_token{lo}")
+            for c in range(0, hi - lo, P):
+                block = (lo + c) // P
+                nc.scalar.activation(by_token[:, c : c + P], turned[:, c : c + P], ACT.Copy, scale=gate_cols[:, block : block + 1])
             back = psum.tile([P, hi - lo], F32, name="bank", bufs=8)
             for c in range(0, hi - lo, P):
                 nc.tensor.transpose(back[:, c : c + P], by_token[:, c : c + P], ident[:])
-            total = keep.tile([P, hi - lo], F32, name=f"total{lo}")
-            nc.scalar.activation(total[:], back[:], ACT.Copy)
-            nc.scalar.dma_start(out=out[:, lo:hi], in_=total[:])
+            return back
 
-        def add_on_vector(first, second, lo, hi):
+        def add_and_store(first, second, lo, hi):
             total = keep.tile([P, hi - lo], F32, name=f"total{lo}")
-            nc.vector.tensor_tensor(total[:], first[:], second[:], ADD)
+            nc.vector.tensor_tensor(total[:], first, second, ADD)
             nc.sync.dma_start(out=out[:, lo:hi], in_=total[:])
 
-        waiting = None
-        first, second = fetch(0, 0, 640), fetch(1, 0, 640)
-        for lo, hi in ((0, 256), (256, 512), (512, 640)):
-            summed = (turn_and_add(first, second, lo, hi), lo, hi)
-            if waiting:
-                turn_back(*waiting)
-            waiting = summed
-        turn_back(*waiting)
-        for lo, hi in ((640, 1152), (1152, 1408), (1408, T)):
-            add_on_vector(fetch(0, lo, hi), fetch(1, lo, hi), lo, hi)
+        pieces = spans(PIECES)
+        firsts = [fetch(0, lo, hi) for lo, hi in pieces]
+        turned = fetch_and_turn(*pieces[0])
+        backs = []
+        for i, (lo, hi) in enumerate(pieces):
+            ahead = fetch_and_turn(*pieces[i + 1]) if i + 1 < len(pieces) else None
+            backs.append(weigh_and_turn_back(turned, lo, hi))
+            turned = ahead
+        add_and_store(fetch(0, TURNED, T)[:], fetch(1, TURNED, T)[:], TURNED, T)
+        for (lo, hi), first, back in zip(pieces, firsts, backs):
+            add_and_store(first[:], back[:], lo, hi)

@@ -31,7 +31,10 @@ SHARES = ((512, 256), (0, 0, 256), (0, 0, 256))
 UNITS = ((256, 256, 512, 128, 128, 256), (512, 512, 128, 128, 256), (512, 512, 128, 128, 256))
 
 
-PIECES = (256, 256, 256, 256, 256)
+BYTE_CUTS = (768, 512, 512, 256)
+WORD_CUTS = (768, 512, 256, 256, 256)
+PIECES = (256, 256, 256, 128)
+PLAIN_PIECES = (256, 256, 128)
 TURNED = sum(PIECES)
 
 
@@ -56,8 +59,8 @@ def tile_moe_cap2_lin_relu2_kernel(tc, xT, w_words, w_scales, b, gate, offs, pos
         w_sb = keep.tile([P, E * PASSES, N], U32, name="w_sb", align_bytes=64)
         w_planes = keep.tile([P, E * PASSES, N], U8, name="w_planes", align_bytes=64)
         b_sb = keep.tile([P, E], F32, name="b_sb")
-        first_col = (0, TURNED)
-        gate_sb = [keep.tile([P, T - first_col[g]], F32, name=f"gate_sb{g}") for g in range(2)]
+        gate_first = keep.tile([P, T - TURNED], F32, name="gate_first")
+        gate_second = keep.tile([P, T], F32, name="gate_second")
         gate_rows = keep.tile([P, P], F32, name="gate_rows")
         gate_cols = keep.tile([P, TURNED // P], F32, name="gate_cols")
         y = keep.tile([P, S + PAD], F32, name="y")
@@ -91,9 +94,9 @@ def tile_moe_cap2_lin_relu2_kernel(tc, xT, w_words, w_scales, b, gate, offs, pos
             )
         nc.sync.dma_start(pos1_sb[:], pos1)
         nc.sync.dma_start(pos2_sb[:], pos2)
-        nc.sync.dma_start(out=gate_rows[: TURNED // P, :], in_=gate[1, 0, :TURNED].rearrange("(c t) -> c t", t=P))
-        for g in range(2):
-            nc.sync.dma_start(out=gate_sb[g][:], in_=gate[g, :, first_col[g] :])
+        nc.sync.dma_start(out=gate_rows[: TURNED // P, :], in_=gate[0, 0, :TURNED].rearrange("(c t) -> c t", t=P))
+        nc.sync.dma_start(out=gate_second[:], in_=gate[1])
+        nc.sync.dma_start(out=gate_first[:], in_=gate[0, :, TURNED:])
 
         for a in range(PASSES):
             for u0, u1 in spans(UNITS[a]):
@@ -140,11 +143,12 @@ def tile_moe_cap2_lin_relu2_kernel(tc, xT, w_words, w_scales, b, gate, offs, pos
 
         all_groups = [(e * C, C) for e in range(E - 1)] + [(S - C, P), (S - P, P)]
         banks = {}
-        for lo, hi in ((0, 768), (768, 1536), (1536, 1792), (1792, 2048)):
-            if lo % T == 0:
-                gather(slot_planes, planes[:], lo, min(lo + T, S))
+        byte_cuts = dict(spans(BYTE_CUTS))
+        for lo, hi in spans(WORD_CUTS):
+            if lo in byte_cuts:
+                gather(slot_planes, planes[:], lo, byte_cuts[lo])
                 for first, width in all_groups:
-                    if lo <= first < lo + T:
+                    if lo <= first < byte_cuts[lo]:
                         banks[first] = psum.tile([P, width], F32, name="bank", bufs=8)
                         for a in range(PASSES - 1):
                             multiply(banks[first], first, width, a)
@@ -166,22 +170,24 @@ def tile_moe_cap2_lin_relu2_kernel(tc, xT, w_words, w_scales, b, gate, offs, pos
                 else:
                     nc.vector.tensor_tensor(y[:, first : first + width], relu[:], relu[:], MULT)
 
-        def fetch(g, lo, hi):
-            z = keep.tile([P, hi - lo], F32, name=f"z{g}_{lo}")
-            pos_sb = (pos1_sb, pos2_sb)[g]
-            nc.vector.tensor_tensor(z[:], y[:].indirect(pos_sb[:, lo // 16 : hi // 16]), gate_sb[g][:, lo - first_col[g] : hi - first_col[g]], MULT)
+        def fetch_second(lo, hi):
+            z = keep.tile([P, hi - lo], F32, name=f"second{lo}")
+            nc.vector.tensor_tensor(z[:], y[:].indirect(pos2_sb[:, lo // 16 : hi // 16]), gate_second[:, lo:hi], MULT)
             return z
+
+        def fetch_first(z, lo, hi):
+            nc.scalar.activation(z[:], y[:].indirect(pos1_sb[:, lo // 16 : hi // 16]), ACT.Copy)
 
         def fetch_and_turn(lo, hi):
             plain = keep.tile([P, hi - lo], F32, name=f"plain{lo}")
-            nc.scalar.activation(plain[:], y[:].indirect(pos2_sb[:, lo // 16 : hi // 16]), ACT.Copy)
+            fetch_first(plain, lo, hi)
             turned = psum.tile([P, hi - lo], F32, name="bank", bufs=8)
             for c in range(0, hi - lo, P):
                 nc.tensor.transpose(turned[:, c : c + P], plain[:, c : c + P], ident[:])
             return turned
 
         def weigh_and_turn_back(turned, lo, hi):
-            by_token = keep.tile([P, hi - lo], F32, name=f"by_token{lo}")
+            by_token = keep.tile([P, hi - lo], F32, name="staged", bufs=len(PIECES))
             for c in range(0, hi - lo, P):
                 block = (lo + c) // P
                 nc.scalar.activation(by_token[:, c : c + P], turned[:, c : c + P], ACT.Copy, scale=gate_cols[:, block : block + 1])
@@ -196,13 +202,15 @@ def tile_moe_cap2_lin_relu2_kernel(tc, xT, w_words, w_scales, b, gate, offs, pos
             nc.sync.dma_start(out=out[:, lo:hi], in_=total[:])
 
         pieces = spans(PIECES)
-        firsts = [fetch(0, lo, hi) for lo, hi in pieces]
-        turned = fetch_and_turn(*pieces[0])
-        backs = []
-        for i, (lo, hi) in enumerate(pieces):
-            ahead = fetch_and_turn(*pieces[i + 1]) if i + 1 < len(pieces) else None
-            backs.append(weigh_and_turn_back(turned, lo, hi))
-            turned = ahead
-        add_and_store(fetch(0, TURNED, T)[:], fetch(1, TURNED, T)[:], TURNED, T)
-        for (lo, hi), first, back in zip(pieces, firsts, backs):
-            add_and_store(first[:], back[:], lo, hi)
+        plain_pieces = [(TURNED + lo, TURNED + hi) for lo, hi in spans(PLAIN_PIECES)]
+        turned_second, plain_second = fetch_second(0, TURNED), fetch_second(TURNED, T)
+        turned = [fetch_and_turn(lo, hi) for lo, hi in pieces]
+        backs = [weigh_and_turn_back(bank, lo, hi) for bank, (lo, hi) in zip(turned, pieces)]
+        for (lo, hi), back in zip(pieces, backs):
+            add_and_store(back[:], turned_second[:, lo:hi], lo, hi)
+        for lo, hi in plain_pieces:
+            plain = keep.tile([P, hi - lo], F32, name="staged", bufs=len(PIECES))
+            fetch_first(plain, lo, hi)
+            first = keep.tile([P, hi - lo], F32, name=f"first{lo}")
+            nc.vector.tensor_tensor(first[:], plain[:], gate_first[:, lo - TURNED : hi - TURNED], MULT)
+            add_and_store(first[:], plain_second[:, lo - TURNED : hi - TURNED], lo, hi)

@@ -34,7 +34,7 @@ UNITS = ((256, 256, 512, 128, 128, 256), (512, 512, 128, 128, 256), (512, 512, 1
 BYTE_CUTS = (768, 512, 512, 256)
 WORD_CUTS = (768, 512, 256, 256, 256)
 PIECES = (256, 256, 256, 128)
-PLAIN_PIECES = (256, 256, 128)
+PLAIN_PIECES = (256, 256)
 TURNED = sum(PIECES)
 
 
@@ -59,8 +59,9 @@ def tile_moe_cap2_lin_relu2_kernel(tc, xT, w_words, w_scales, b, gate, offs, pos
         w_sb = keep.tile([P, E * PASSES, N], U32, name="w_sb", align_bytes=64)
         w_planes = keep.tile([P, E * PASSES, N], U8, name="w_planes", align_bytes=64)
         b_sb = keep.tile([P, E], F32, name="b_sb")
-        gate_first = keep.tile([P, T - TURNED], F32, name="gate_first")
-        gate_second = keep.tile([P, T], F32, name="gate_second")
+        pos_sb = (pos1_sb, pos2_sb)
+        first_col = (TURNED, 0)
+        gate_sb = [keep.tile([P, T - first_col[g]], F32, name=f"gate_sb{g}") for g in range(2)]
         gate_rows = keep.tile([P, P], F32, name="gate_rows")
         gate_cols = keep.tile([P, TURNED // P], F32, name="gate_cols")
         y = keep.tile([P, S + PAD], F32, name="y")
@@ -95,8 +96,8 @@ def tile_moe_cap2_lin_relu2_kernel(tc, xT, w_words, w_scales, b, gate, offs, pos
         nc.sync.dma_start(pos1_sb[:], pos1)
         nc.sync.dma_start(pos2_sb[:], pos2)
         nc.sync.dma_start(out=gate_rows[: TURNED // P, :], in_=gate[0, 0, :TURNED].rearrange("(c t) -> c t", t=P))
-        nc.sync.dma_start(out=gate_second[:], in_=gate[1])
-        nc.sync.dma_start(out=gate_first[:], in_=gate[0, :, TURNED:])
+        for g in (1, 0):
+            nc.sync.dma_start(out=gate_sb[g][:], in_=gate[g, :, first_col[g] :])
 
         for a in range(PASSES):
             for u0, u1 in spans(UNITS[a]):
@@ -170,17 +171,17 @@ def tile_moe_cap2_lin_relu2_kernel(tc, xT, w_words, w_scales, b, gate, offs, pos
                 else:
                     nc.vector.tensor_tensor(y[:, first : first + width], relu[:], relu[:], MULT)
 
-        def fetch_second(lo, hi):
-            z = keep.tile([P, hi - lo], F32, name=f"second{lo}")
-            nc.vector.tensor_tensor(z[:], y[:].indirect(pos2_sb[:, lo // 16 : hi // 16]), gate_second[:, lo:hi], MULT)
+        def fetch_weighed(g, lo, hi):
+            z = keep.tile([P, hi - lo], F32, name=f"weighed{g}_{lo}")
+            nc.vector.tensor_tensor(z[:], y[:].indirect(pos_sb[g][:, lo // 16 : hi // 16]), gate_sb[g][:, lo - first_col[g] : hi - first_col[g]], MULT)
             return z
 
-        def fetch_first(z, lo, hi):
-            nc.scalar.activation(z[:], y[:].indirect(pos1_sb[:, lo // 16 : hi // 16]), ACT.Copy)
+        def fetch_plain(z, g, lo, hi):
+            nc.scalar.activation(z[:], y[:].indirect(pos_sb[g][:, lo // 16 : hi // 16]), ACT.Copy)
 
         def fetch_and_turn(lo, hi):
             plain = keep.tile([P, hi - lo], F32, name=f"plain{lo}")
-            fetch_first(plain, lo, hi)
+            fetch_plain(plain, 0, lo, hi)
             turned = psum.tile([P, hi - lo], F32, name="bank", bufs=8)
             for c in range(0, hi - lo, P):
                 nc.tensor.transpose(turned[:, c : c + P], plain[:, c : c + P], ident[:])
@@ -203,14 +204,17 @@ def tile_moe_cap2_lin_relu2_kernel(tc, xT, w_words, w_scales, b, gate, offs, pos
 
         pieces = spans(PIECES)
         plain_pieces = [(TURNED + lo, TURNED + hi) for lo, hi in spans(PLAIN_PIECES)]
-        turned_second, plain_second = fetch_second(0, TURNED), fetch_second(TURNED, T)
+        shared_end = plain_pieces[-1][1]
+        turned_second, plain_first = fetch_weighed(1, 0, TURNED), fetch_weighed(0, TURNED, T)
+        last_second = fetch_weighed(1, shared_end, T)
         turned = [fetch_and_turn(lo, hi) for lo, hi in pieces]
         backs = [weigh_and_turn_back(bank, lo, hi) for bank, (lo, hi) in zip(turned, pieces)]
+        add_and_store(plain_first[:, shared_end - TURNED :], last_second[:], shared_end, T)
         for (lo, hi), back in zip(pieces, backs):
             add_and_store(back[:], turned_second[:, lo:hi], lo, hi)
         for lo, hi in plain_pieces:
             plain = keep.tile([P, hi - lo], F32, name="staged", bufs=len(PIECES))
-            fetch_first(plain, lo, hi)
-            first = keep.tile([P, hi - lo], F32, name=f"first{lo}")
-            nc.vector.tensor_tensor(first[:], plain[:], gate_first[:, lo - TURNED : hi - TURNED], MULT)
-            add_and_store(first[:], plain_second[:, lo - TURNED : hi - TURNED], lo, hi)
+            fetch_plain(plain, 1, lo, hi)
+            second = keep.tile([P, hi - lo], F32, name=f"second{lo}")
+            nc.vector.tensor_tensor(second[:], plain[:], gate_sb[1][:, lo:hi], MULT)
+            add_and_store(second[:], plain_first[:, lo - TURNED : hi - TURNED], lo, hi)

@@ -26,9 +26,9 @@ MULT = mybir.AluOpType.mult
 ADD = mybir.AluOpType.add
 MAX = mybir.AluOpType.max
 
-LOADS = ((1024, 512), (512, 512, 512), (512, 512, 512))
-SHARES = ((512, 256), (0, 0, 256), (0, 0, 256))
-UNITS = ((256, 256, 512, 128, 128, 256), (512, 512, 128, 128, 256), (512, 512, 128, 128, 256))
+LOADS = ((1024, 512), (768, 768), (512, 512, 512))
+SHARES = ((512, 256), (0, 384), (0, 0, 256))
+UNITS = ((256, 256, 512, 128, 128, 256), (512, 256, 256, 128, 128, 256), (512, 512, 128, 128, 256))
 
 
 BYTE_CUTS = (768, 512, 512, 256)

@@ -107,8 +107,9 @@ def tile_moe_cap2_lin_relu2_kernel(tc, xT, w_words, w_scales, b, gate, offs, pos
                         lo, hi = max(lo, u0), min(hi, u1)
                         if lo >= hi:
                             continue
-                        dst = grouped[:, lo - u0 : hi - u0, :].rearrange("p (c i) j -> p c j i", i=4)
-                        source = raws[a, l0][:, :, lo - l0 : hi - l0].rearrange("p j (c i) -> p c j i", i=4)
+                        run = 4 if on_vector else 2
+                        dst = grouped[:, lo - u0 : hi - u0, :].rearrange("p (c i) j -> p c j i", i=run)
+                        source = raws[a, l0][:, :, lo - l0 : hi - l0].rearrange("p j (c i) -> p c j i", i=run)
                         if on_vector:
                             nc.vector.tensor_copy(dst, source)
                         else:

@@ -11,6 +11,7 @@ PACK = 4
 K_PASS = P * PACK
 PASSES = K // K_PASS
 WIDE = 2 * S
+BANK = 512
 
 FLOPS = 2 * K * N * S
 
@@ -29,17 +30,18 @@ MAX = mybir.AluOpType.max
 LOADS = ((1024, 512), (768, 768), (512, 512, 512))
 SHARES = ((512, 256), (0, 384), (0, 0, 256))
 UNITS = ((256, 256, 512, 128, 128, 256), (512, 256, 256, 128, 128, 256), (512, 512, 128, 128, 256))
-
-
 BYTE_CUTS = (768, 512, 512, 256)
 WORD_CUTS = (768, 512, 256, 256, 256)
-PIECES = (256, 256, 256, 128)
-PLAIN_PIECES = (256, 256)
-TURNED = sum(PIECES)
+TURNED_PIECES = (256, 256, 128)
+PLAIN_PIECES = (256, 256, 128, 128)
+TURNED = sum(TURNED_PIECES)
+PLAIN = sum(PLAIN_PIECES)
+TURNED_FROM = T - TURNED
+GATE_ROWS = (TURNED + PLAIN) // P
 
 
-def spans(widths):
-    return [(sum(widths[:i]), sum(widths[: i + 1])) for i in range(len(widths))]
+def spans(widths, first=0):
+    return [(first + sum(widths[:i]), first + sum(widths[: i + 1])) for i in range(len(widths))]
 
 
 def tile_moe_cap2_lin_relu2_kernel(tc, xT, w_words, w_scales, b, gate, offs, pos1, pos2, out):
@@ -49,8 +51,7 @@ def tile_moe_cap2_lin_relu2_kernel(tc, xT, w_words, w_scales, b, gate, offs, pos
         psum = ctx.enter_context(tc.psum_pool(name="psum", bufs=1))
 
         offs_sb = keep.tile([P, S // 16], U16, name="offs_sb")
-        pos1_sb = keep.tile([P, T // 16], U16, name="pos1_sb")
-        pos2_sb = keep.tile([P, T // 16], U16, name="pos2_sb")
+        pos_sb = [keep.tile([P, T // 16], U16, name=f"pos_sb{g}") for g in range(2)]
         all_codes = keep.tile([P, (PASSES - 1) * T + WIDE], U32, name="all_codes", align_bytes=64)
         codes = [all_codes[:, (PASSES - 1 - a) * T :] for a in range(PASSES)]
         planes = keep.tile([P, S], U8, name="planes", align_bytes=64)
@@ -59,11 +60,11 @@ def tile_moe_cap2_lin_relu2_kernel(tc, xT, w_words, w_scales, b, gate, offs, pos
         w_sb = keep.tile([P, E * PASSES, N], U32, name="w_sb", align_bytes=64)
         w_planes = keep.tile([P, E * PASSES, N], U8, name="w_planes", align_bytes=64)
         b_sb = keep.tile([P, E], F32, name="b_sb")
-        pos_sb = (pos1_sb, pos2_sb)
-        first_col = (TURNED, 0)
-        gate_sb = [keep.tile([P, T - first_col[g]], F32, name=f"gate_sb{g}") for g in range(2)]
+        gate_first = keep.tile([P, TURNED_FROM], F32, name="gate_first")
+        gate_turned = keep.tile([P, TURNED], F32, name="gate_turned")
+        gate_last = keep.tile([P, TURNED_FROM - PLAIN], F32, name="gate_last")
         gate_rows = keep.tile([P, P], F32, name="gate_rows")
-        gate_cols = keep.tile([P, TURNED // P], F32, name="gate_cols")
+        gate_cols = keep.tile([P, GATE_ROWS], F32, name="gate_cols")
         y = keep.tile([P, S + PAD], F32, name="y")
         zeros = keep.tile([P, PAD], F32, name="zeros")
         ident = keep.tile([P, P], F32, name="ident")
@@ -88,16 +89,19 @@ def tile_moe_cap2_lin_relu2_kernel(tc, xT, w_words, w_scales, b, gate, offs, pos
         scale_rows = w_scales.rearrange("e a (q r) n -> r q (e a) n", r=4)
         for r in range(4):
             nc.sync.dma_start(out=w_planes[r:P:32].bitcast(I32), in_=scale_rows[r].bitcast(I32))
+        gate_blocks = gate.rearrange("g n (c t) -> (g n c) t", t=P)
+        seam = N * T // P
+        nc.sync.dma_start(out=gate_rows[:GATE_ROWS, :], in_=gate_blocks[seam - TURNED // P : seam + PLAIN // P, :])
         for e in range(0, E, 2):
             nc.sync.dma_start(
                 out=w_sb[:, e * PASSES : (e + 2) * PASSES, :].bitcast(I32),
                 in_=w_words[e : e + 2].rearrange("e a p n r -> p (e a) (n r)").bitcast(I32),
             )
-        nc.sync.dma_start(pos1_sb[:], pos1)
-        nc.sync.dma_start(pos2_sb[:], pos2)
-        nc.sync.dma_start(out=gate_rows[: TURNED // P, :], in_=gate[0, 0, :TURNED].rearrange("(c t) -> c t", t=P))
-        for g in (1, 0):
-            nc.sync.dma_start(out=gate_sb[g][:], in_=gate[g, :, first_col[g] :])
+        nc.sync.dma_start(pos_sb[0][:], pos1)
+        nc.sync.dma_start(pos_sb[1][:], pos2)
+        nc.sync.dma_start(out=gate_last[:], in_=gate[1, :, PLAIN:TURNED_FROM])
+        nc.sync.dma_start(out=gate_first[:], in_=gate[0, :, :TURNED_FROM])
+        nc.sync.dma_start(out=gate_turned[:], in_=gate[1, :, TURNED_FROM:])
 
         for a in range(PASSES):
             for u0, u1 in spans(UNITS[a]):
@@ -126,9 +130,13 @@ def tile_moe_cap2_lin_relu2_kernel(tc, xT, w_words, w_scales, b, gate, offs, pos
         for a in range(PASSES - 1):
             gather(slot_codes[a], codes[a][:, :WIDE], 0, S)
 
-        gate_bank = psum.tile([P, P], F32, name="bank", bufs=8)
+        gate_bank = psum.tile([P, P], F32, name="bank", bufs=6)
         nc.tensor.transpose(gate_bank[:], gate_rows[:], ident[:])
-        nc.scalar.activation(gate_cols[:], gate_bank[:, : TURNED // P], ACT.Copy)
+        nc.scalar.activation(gate_cols[:], gate_bank[:, :GATE_ROWS], ACT.Copy)
+        spread = [psum.tile([P, min(BANK, PLAIN - lo)], F32, name="spread", bufs=2) for lo in range(0, PLAIN, BANK)]
+        for c in range(0, PLAIN, P):
+            column = gate_cols[:, (TURNED + c) // P : (TURNED + c) // P + 1]
+            nc.tensor.transpose(spread[c // BANK][:, c % BANK : c % BANK + P], column.to_broadcast([P, P]), ident[:])
 
         def multiply(acc, first, width, a):
             e = first // C
@@ -151,7 +159,7 @@ def tile_moe_cap2_lin_relu2_kernel(tc, xT, w_words, w_scales, b, gate, offs, pos
                 gather(slot_planes, planes[:], lo, byte_cuts[lo])
                 for first, width in all_groups:
                     if lo <= first < byte_cuts[lo]:
-                        banks[first] = psum.tile([P, width], F32, name="bank", bufs=8)
+                        banks[first] = psum.tile([P, width], F32, name="bank", bufs=6)
                         for a in range(PASSES - 1):
                             multiply(banks[first], first, width, a)
             gather(slot_codes[PASSES - 1], codes[PASSES - 1][:, :T], lo, hi)
@@ -172,50 +180,59 @@ def tile_moe_cap2_lin_relu2_kernel(tc, xT, w_words, w_scales, b, gate, offs, pos
                 else:
                     nc.vector.tensor_tensor(y[:, first : first + width], relu[:], relu[:], MULT)
 
-        def fetch_weighed(g, lo, hi):
+        def fetch_weighed(g, lo, hi, weights):
             z = keep.tile([P, hi - lo], F32, name=f"weighed{g}_{lo}")
-            nc.vector.tensor_tensor(z[:], y[:].indirect(pos_sb[g][:, lo // 16 : hi // 16]), gate_sb[g][:, lo - first_col[g] : hi - first_col[g]], MULT)
+            nc.vector.tensor_tensor(z[:], y[:].indirect(pos_sb[g][:, lo // 16 : hi // 16]), weights[:], MULT)
             return z
 
         def fetch_plain(z, g, lo, hi):
             nc.scalar.activation(z[:], y[:].indirect(pos_sb[g][:, lo // 16 : hi // 16]), ACT.Copy)
 
         def fetch_and_turn(lo, hi):
-            plain = keep.tile([P, hi - lo], F32, name=f"plain{lo}")
+            plain = keep.tile([P, hi - lo], F32, name="staged", bufs=2)
             fetch_plain(plain, 0, lo, hi)
-            turned = psum.tile([P, hi - lo], F32, name="bank", bufs=8)
+            turned = psum.tile([P, hi - lo], F32, name="bank", bufs=6)
             for c in range(0, hi - lo, P):
                 nc.tensor.transpose(turned[:, c : c + P], plain[:, c : c + P], ident[:])
             return turned
 
         def weigh_and_turn_back(turned, lo, hi):
-            by_token = keep.tile([P, hi - lo], F32, name="staged", bufs=len(PIECES))
+            by_token = keep.tile([P, hi - lo], F32, name=f"by_token{lo}")
             for c in range(0, hi - lo, P):
-                block = (lo + c) // P
+                block = (lo - TURNED_FROM + c) // P
                 nc.scalar.activation(by_token[:, c : c + P], turned[:, c : c + P], ACT.Copy, scale=gate_cols[:, block : block + 1])
-            back = psum.tile([P, hi - lo], F32, name="bank", bufs=8)
+            back = psum.tile([P, hi - lo], F32, name="bank", bufs=6)
             for c in range(0, hi - lo, P):
                 nc.tensor.transpose(back[:, c : c + P], by_token[:, c : c + P], ident[:])
             return back
 
-        def add_and_store(first, second, lo, hi):
+        def add_and_store(engine, first, second, lo, hi):
             total = keep.tile([P, hi - lo], F32, name=f"total{lo}")
-            nc.vector.tensor_tensor(total[:], first, second, ADD)
+            engine.tensor_tensor(total[:], first, second, ADD)
             nc.sync.dma_start(out=out[:, lo:hi], in_=total[:])
 
-        pieces = spans(PIECES)
-        plain_pieces = [(TURNED + lo, TURNED + hi) for lo, hi in spans(PLAIN_PIECES)]
-        shared_end = plain_pieces[-1][1]
-        turned_second, plain_first = fetch_weighed(1, 0, TURNED), fetch_weighed(0, TURNED, T)
-        last_second = fetch_weighed(1, shared_end, T)
-        turned = [fetch_and_turn(lo, hi) for lo, hi in pieces]
-        backs = [weigh_and_turn_back(bank, lo, hi) for bank, (lo, hi) in zip(turned, pieces)]
-        add_and_store(plain_first[:, shared_end - TURNED :], last_second[:], shared_end, T)
+        last_second = fetch_weighed(1, PLAIN, TURNED_FROM, gate_last)
+        later_first = fetch_weighed(0, 0, TURNED_FROM, gate_first)
+        turned_second = fetch_weighed(1, TURNED_FROM, T, gate_turned)
+        plain_second = keep.tile([P, PLAIN], F32, name="plain_second")
+        fetch_plain(plain_second, 1, 0, PLAIN)
+        pieces = spans(TURNED_PIECES, TURNED_FROM)
+        turned, backs = [], []
+        for i in range(len(pieces) + 1):
+            if i < len(pieces):
+                turned.append(fetch_and_turn(*pieces[i]))
+            if i > 0:
+                backs.append(weigh_and_turn_back(turned[i - 1], *pieces[i - 1]))
+
+        add_and_store(nc.gpsimd, later_first[:, PLAIN:], last_second[:], PLAIN, TURNED_FROM)
+        products = []
+        for lo, hi in spans(PLAIN_PIECES):
+            product = keep.tile([P, hi - lo], F32, name=f"product{lo}")
+            nc.vector.tensor_tensor(product[:], spread[lo // BANK][:, lo % BANK : lo % BANK + hi - lo], plain_second[:, lo:hi], MULT)
+            products.append(product)
+        for (lo, hi), product in list(zip(spans(PLAIN_PIECES), products))[:-1]:
+            add_and_store(nc.gpsimd, product[:], later_first[:, lo:hi], lo, hi)
         for (lo, hi), back in zip(pieces, backs):
-            add_and_store(back[:], turned_second[:, lo:hi], lo, hi)
-        for lo, hi in plain_pieces:
-            plain = keep.tile([P, hi - lo], F32, name="staged", bufs=len(PIECES))
-            fetch_plain(plain, 1, lo, hi)
-            second = keep.tile([P, hi - lo], F32, name=f"second{lo}")
-            nc.vector.tensor_tensor(second[:], plain[:], gate_sb[1][:, lo:hi], MULT)
-            add_and_store(second[:], plain_first[:, lo - TURNED : hi - TURNED], lo, hi)
+            add_and_store(nc.vector, back[:], turned_second[:, lo - TURNED_FROM : hi - TURNED_FROM], lo, hi)
+        lo, hi = spans(PLAIN_PIECES)[-1]
+        add_and_store(nc.vector, products[-1][:], later_first[:, lo:hi], lo, hi)

@@ -32,12 +32,12 @@ SHARES = ((512, 256), (0, 384), (0, 0, 256))
 UNITS = ((256, 256, 512, 128, 128, 256), (512, 256, 256, 128, 128, 256), (512, 512, 128, 128, 256))
 BYTE_CUTS = (768, 512, 512, 256)
 WORD_CUTS = (768, 512, 256, 256, 256)
-TURNED_PIECES = (256, 256, 128)
-PLAIN_PIECES = (256, 256, 128, 128)
+TURNED_PIECES = (256, 256, 256, 128)
+PLAIN_PIECES = (256, 256)
 TURNED = sum(TURNED_PIECES)
 PLAIN = sum(PLAIN_PIECES)
 TURNED_FROM = T - TURNED
-GATE_ROWS = (TURNED + PLAIN) // P
+GATE_ROWS = TURNED // P
 
 
 def spans(widths, first=0):
@@ -62,7 +62,7 @@ def tile_moe_cap2_lin_relu2_kernel(tc, xT, w_words, w_scales, b, gate, offs, pos
         b_sb = keep.tile([P, E], F32, name="b_sb")
         gate_first = keep.tile([P, TURNED_FROM], F32, name="gate_first")
         gate_turned = keep.tile([P, TURNED], F32, name="gate_turned")
-        gate_last = keep.tile([P, TURNED_FROM - PLAIN], F32, name="gate_last")
+        gate_last = keep.tile([P, TURNED_FROM], F32, name="gate_last")
         gate_rows = keep.tile([P, P], F32, name="gate_rows")
         gate_cols = keep.tile([P, GATE_ROWS], F32, name="gate_cols")
         y = keep.tile([P, S + PAD], F32, name="y")
@@ -89,9 +89,7 @@ def tile_moe_cap2_lin_relu2_kernel(tc, xT, w_words, w_scales, b, gate, offs, pos
         scale_rows = w_scales.rearrange("e a (q r) n -> r q (e a) n", r=4)
         for r in range(4):
             nc.sync.dma_start(out=w_planes[r:P:32].bitcast(I32), in_=scale_rows[r].bitcast(I32))
-        gate_blocks = gate.rearrange("g n (c t) -> (g n c) t", t=P)
-        seam = N * T // P
-        nc.sync.dma_start(out=gate_rows[:GATE_ROWS, :], in_=gate_blocks[seam - TURNED // P : seam + PLAIN // P, :])
+        nc.sync.dma_start(out=gate_rows[:GATE_ROWS, :], in_=gate[0, 0, TURNED_FROM:].rearrange("(c t) -> c t", t=P))
         for e in range(0, E, 2):
             nc.sync.dma_start(
                 out=w_sb[:, e * PASSES : (e + 2) * PASSES, :].bitcast(I32),
@@ -99,7 +97,7 @@ def tile_moe_cap2_lin_relu2_kernel(tc, xT, w_words, w_scales, b, gate, offs, pos
             )
         nc.sync.dma_start(pos_sb[0][:], pos1)
         nc.sync.dma_start(pos_sb[1][:], pos2)
-        nc.sync.dma_start(out=gate_last[:], in_=gate[1, :, PLAIN:TURNED_FROM])
+        nc.sync.dma_start(out=gate_last[:], in_=gate[1, :, :TURNED_FROM])
         nc.sync.dma_start(out=gate_first[:], in_=gate[0, :, :TURNED_FROM])
         nc.sync.dma_start(out=gate_turned[:], in_=gate[1, :, TURNED_FROM:])
 
@@ -130,13 +128,9 @@ def tile_moe_cap2_lin_relu2_kernel(tc, xT, w_words, w_scales, b, gate, offs, pos
         for a in range(PASSES - 1):
             gather(slot_codes[a], codes[a][:, :WIDE], 0, S)
 
-        gate_bank = psum.tile([P, P], F32, name="bank", bufs=6)
+        gate_bank = psum.tile([P, P], F32, name="bank", bufs=8)
         nc.tensor.transpose(gate_bank[:], gate_rows[:], ident[:])
         nc.scalar.activation(gate_cols[:], gate_bank[:, :GATE_ROWS], ACT.Copy)
-        spread = [psum.tile([P, min(BANK, PLAIN - lo)], F32, name="spread", bufs=2) for lo in range(0, PLAIN, BANK)]
-        for c in range(0, PLAIN, P):
-            column = gate_cols[:, (TURNED + c) // P : (TURNED + c) // P + 1]
-            nc.tensor.transpose(spread[c // BANK][:, c % BANK : c % BANK + P], column.to_broadcast([P, P]), ident[:])
 
         def multiply(acc, first, width, a):
             e = first // C
@@ -159,7 +153,7 @@ def tile_moe_cap2_lin_relu2_kernel(tc, xT, w_words, w_scales, b, gate, offs, pos
                 gather(slot_planes, planes[:], lo, byte_cuts[lo])
                 for first, width in all_groups:
                     if lo <= first < byte_cuts[lo]:
-                        banks[first] = psum.tile([P, width], F32, name="bank", bufs=6)
+                        banks[first] = psum.tile([P, width], F32, name="bank", bufs=8)
                         for a in range(PASSES - 1):
                             multiply(banks[first], first, width, a)
             gather(slot_codes[PASSES - 1], codes[PASSES - 1][:, :T], lo, hi)
@@ -182,16 +176,16 @@ def tile_moe_cap2_lin_relu2_kernel(tc, xT, w_words, w_scales, b, gate, offs, pos
 
         def fetch_weighed(g, lo, hi, weights):
             z = keep.tile([P, hi - lo], F32, name=f"weighed{g}_{lo}")
-            nc.vector.tensor_tensor(z[:], y[:].indirect(pos_sb[g][:, lo // 16 : hi // 16]), weights[:], MULT)
+            nc.vector.tensor_tensor(z[:], y[:].indirect(pos_sb[g][:, lo // 16 : hi // 16]), weights, MULT)
             return z
 
         def fetch_plain(z, g, lo, hi):
             nc.scalar.activation(z[:], y[:].indirect(pos_sb[g][:, lo // 16 : hi // 16]), ACT.Copy)
 
         def fetch_and_turn(lo, hi):
-            plain = keep.tile([P, hi - lo], F32, name="staged", bufs=2)
+            plain = keep.tile([P, hi - lo], F32, name=f"plain{lo}")
             fetch_plain(plain, 0, lo, hi)
-            turned = psum.tile([P, hi - lo], F32, name="bank", bufs=6)
+            turned = psum.tile([P, hi - lo], F32, name="bank", bufs=8)
             for c in range(0, hi - lo, P):
                 nc.tensor.transpose(turned[:, c : c + P], plain[:, c : c + P], ident[:])
             return turned
@@ -201,7 +195,7 @@ def tile_moe_cap2_lin_relu2_kernel(tc, xT, w_words, w_scales, b, gate, offs, pos
             for c in range(0, hi - lo, P):
                 block = (lo - TURNED_FROM + c) // P
                 nc.scalar.activation(by_token[:, c : c + P], turned[:, c : c + P], ACT.Copy, scale=gate_cols[:, block : block + 1])
-            back = psum.tile([P, hi - lo], F32, name="bank", bufs=6)
+            back = psum.tile([P, hi - lo], F32, name="bank", bufs=8)
             for c in range(0, hi - lo, P):
                 nc.tensor.transpose(back[:, c : c + P], by_token[:, c : c + P], ident[:])
             return back
@@ -211,28 +205,21 @@ def tile_moe_cap2_lin_relu2_kernel(tc, xT, w_words, w_scales, b, gate, offs, pos
             engine.tensor_tensor(total[:], first, second, ADD)
             nc.sync.dma_start(out=out[:, lo:hi], in_=total[:])
 
-        last_second = fetch_weighed(1, PLAIN, TURNED_FROM, gate_last)
-        later_first = fetch_weighed(0, 0, TURNED_FROM, gate_first)
-        turned_second = fetch_weighed(1, TURNED_FROM, T, gate_turned)
+        last_second = fetch_weighed(1, PLAIN, TURNED_FROM, gate_last[:, PLAIN:])
+        later_first = fetch_weighed(0, 0, TURNED_FROM, gate_first[:])
         plain_second = keep.tile([P, PLAIN], F32, name="plain_second")
         fetch_plain(plain_second, 1, 0, PLAIN)
-        pieces = spans(TURNED_PIECES, TURNED_FROM)
-        turned, backs = [], []
-        for i in range(len(pieces) + 1):
-            if i < len(pieces):
-                turned.append(fetch_and_turn(*pieces[i]))
-            if i > 0:
-                backs.append(weigh_and_turn_back(turned[i - 1], *pieces[i - 1]))
-
-        add_and_store(nc.gpsimd, later_first[:, PLAIN:], last_second[:], PLAIN, TURNED_FROM)
         products = []
         for lo, hi in spans(PLAIN_PIECES):
             product = keep.tile([P, hi - lo], F32, name=f"product{lo}")
-            nc.vector.tensor_tensor(product[:], spread[lo // BANK][:, lo % BANK : lo % BANK + hi - lo], plain_second[:, lo:hi], MULT)
+            nc.vector.tensor_tensor(product[:], plain_second[:, lo:hi], gate_last[:, lo:hi], MULT)
             products.append(product)
-        for (lo, hi), product in list(zip(spans(PLAIN_PIECES), products))[:-1]:
-            add_and_store(nc.gpsimd, product[:], later_first[:, lo:hi], lo, hi)
+        add_and_store(nc.vector, later_first[:, PLAIN:], last_second[:], PLAIN, TURNED_FROM)
+        for (lo, hi), product in zip(spans(PLAIN_PIECES), products):
+            add_and_store(nc.vector, product[:], later_first[:, lo:hi], lo, hi)
+        turned_second = fetch_weighed(1, TURNED_FROM, T, gate_turned[:])
+        pieces = spans(TURNED_PIECES, TURNED_FROM)
+        turned = [fetch_and_turn(lo, hi) for lo, hi in pieces]
+        backs = [weigh_and_turn_back(bank, lo, hi) for bank, (lo, hi) in zip(turned, pieces)]
         for (lo, hi), back in zip(pieces, backs):
             add_and_store(nc.vector, back[:], turned_second[:, lo - TURNED_FROM : hi - TURNED_FROM], lo, hi)
-        lo, hi = spans(PLAIN_PIECES)[-1]
-        add_and_store(nc.vector, products[-1][:], later_first[:, lo:hi], lo, hi)

@@ -31,9 +31,9 @@ LOADS = ((1024, 512), (768, 768), (512, 512, 512))
 SHARES = ((512, 256), (0, 384), (0, 0, 256))
 UNITS = ((256, 256, 512, 128, 128, 256), (512, 256, 256, 128, 128, 256), (512, 512, 128, 128, 256))
 BYTE_CUTS = (768, 512, 512, 256)
-WORD_CUTS = (768, 512, 256, 256, 256)
-TURNED_PIECES = (256, 256, 256, 128)
-PLAIN_PIECES = (256, 256)
+WORD_CUTS = (768, 512, 256, 256, 128, 128)
+TURNED_PIECES = (256, 256, 256)
+PLAIN_PIECES = (256, 256, 128)
 TURNED = sum(TURNED_PIECES)
 PLAIN = sum(PLAIN_PIECES)
 TURNED_FROM = T - TURNED
@@ -52,8 +52,9 @@ def tile_moe_cap2_lin_relu2_kernel(tc, xT, w_words, w_scales, b, gate, offs, pos
 
         offs_sb = keep.tile([P, S // 16], U16, name="offs_sb")
         pos_sb = [keep.tile([P, T // 16], U16, name=f"pos_sb{g}") for g in range(2)]
-        all_codes = keep.tile([P, (PASSES - 1) * T + WIDE], U32, name="all_codes", align_bytes=64)
-        codes = [all_codes[:, (PASSES - 1 - a) * T :] for a in range(PASSES)]
+        early_codes = keep.tile([P, T + WIDE], U32, name="early_codes", align_bytes=64)
+        last_codes = keep.tile([P, T], U32, name="last_codes", align_bytes=64)
+        codes = [early_codes[:, T:], early_codes[:], last_codes[:]]
         planes = keep.tile([P, S], U8, name="planes", align_bytes=64)
         slot_codes = [keep.tile([P, S], U32, name=f"slot_codes{a}", align_bytes=64) for a in range(PASSES)]
         slot_planes = keep.tile([P, S], U8, name="slot_planes", align_bytes=64)
@@ -61,8 +62,7 @@ def tile_moe_cap2_lin_relu2_kernel(tc, xT, w_words, w_scales, b, gate, offs, pos
         w_planes = keep.tile([P, E * PASSES, N], U8, name="w_planes", align_bytes=64)
         b_sb = keep.tile([P, E], F32, name="b_sb")
         gate_first = keep.tile([P, TURNED_FROM], F32, name="gate_first")
-        gate_turned = keep.tile([P, TURNED], F32, name="gate_turned")
-        gate_last = keep.tile([P, TURNED_FROM], F32, name="gate_last")
+        gate_second = keep.tile([P, T], F32, name="gate_second")
         gate_rows = keep.tile([P, P], F32, name="gate_rows")
         gate_cols = keep.tile([P, GATE_ROWS], F32, name="gate_cols")
         y = keep.tile([P, S + PAD], F32, name="y")
@@ -75,7 +75,7 @@ def tile_moe_cap2_lin_relu2_kernel(tc, xT, w_words, w_scales, b, gate, offs, pos
         nc.vector.memset(gate_rows[:], 0.0)
         nc.vector.memset(w_planes[:].bitcast(I32), 0)
         nc.vector.memset(planes[:].bitcast(I32), 0)
-        nc.vector.memset(all_codes[:, PASSES * T :].bitcast(I32), 0)
+        nc.vector.memset(early_codes[:, 2 * T :].bitcast(I32), 0)
 
         raws = {}
         for a in range(PASSES):
@@ -97,9 +97,8 @@ def tile_moe_cap2_lin_relu2_kernel(tc, xT, w_words, w_scales, b, gate, offs, pos
             )
         nc.sync.dma_start(pos_sb[0][:], pos1)
         nc.sync.dma_start(pos_sb[1][:], pos2)
-        nc.sync.dma_start(out=gate_last[:], in_=gate[1, :, :TURNED_FROM])
+        nc.sync.dma_start(out=gate_second[:], in_=gate[1])
         nc.sync.dma_start(out=gate_first[:], in_=gate[0, :, :TURNED_FROM])
-        nc.sync.dma_start(out=gate_turned[:], in_=gate[1, :, TURNED_FROM:])
 
         for a in range(PASSES):
             for u0, u1 in spans(UNITS[a]):
@@ -156,7 +155,7 @@ def tile_moe_cap2_lin_relu2_kernel(tc, xT, w_words, w_scales, b, gate, offs, pos
                         banks[first] = psum.tile([P, width], F32, name="bank", bufs=8)
                         for a in range(PASSES - 1):
                             multiply(banks[first], first, width, a)
-            gather(slot_codes[PASSES - 1], codes[PASSES - 1][:, :T], lo, hi)
+            gather(slot_codes[PASSES - 1], last_codes[:], lo, hi)
             groups = [(first, width) for first, width in all_groups if lo <= first < hi]
             sums = [banks[first] for first, width in groups]
             for (first, width), acc in zip(groups, sums):
@@ -191,7 +190,7 @@ def tile_moe_cap2_lin_relu2_kernel(tc, xT, w_words, w_scales, b, gate, offs, pos
             return turned
 
         def weigh_and_turn_back(turned, lo, hi):
-            by_token = keep.tile([P, hi - lo], F32, name=f"by_token{lo}")
+            by_token = keep.tile([P, hi - lo], F32, name="staged", bufs=len(TURNED_PIECES))
             for c in range(0, hi - lo, P):
                 block = (lo - TURNED_FROM + c) // P
                 nc.scalar.activation(by_token[:, c : c + P], turned[:, c : c + P], ACT.Copy, scale=gate_cols[:, block : block + 1])
@@ -205,21 +204,18 @@ def tile_moe_cap2_lin_relu2_kernel(tc, xT, w_words, w_scales, b, gate, offs, pos
             engine.tensor_tensor(total[:], first, second, ADD)
             nc.sync.dma_start(out=out[:, lo:hi], in_=total[:])
 
-        last_second = fetch_weighed(1, PLAIN, TURNED_FROM, gate_last[:, PLAIN:])
+        turned_second = fetch_weighed(1, TURNED_FROM, T, gate_second[:, TURNED_FROM:])
         later_first = fetch_weighed(0, 0, TURNED_FROM, gate_first[:])
-        plain_second = keep.tile([P, PLAIN], F32, name="plain_second")
-        fetch_plain(plain_second, 1, 0, PLAIN)
-        products = []
-        for lo, hi in spans(PLAIN_PIECES):
-            product = keep.tile([P, hi - lo], F32, name=f"product{lo}")
-            nc.vector.tensor_tensor(product[:], plain_second[:, lo:hi], gate_last[:, lo:hi], MULT)
-            products.append(product)
-        add_and_store(nc.vector, later_first[:, PLAIN:], last_second[:], PLAIN, TURNED_FROM)
-        for (lo, hi), product in zip(spans(PLAIN_PIECES), products):
-            add_and_store(nc.vector, product[:], later_first[:, lo:hi], lo, hi)
-        turned_second = fetch_weighed(1, TURNED_FROM, T, gate_turned[:])
+        last_second = fetch_weighed(1, PLAIN, TURNED_FROM, gate_second[:, PLAIN:TURNED_FROM])
         pieces = spans(TURNED_PIECES, TURNED_FROM)
         turned = [fetch_and_turn(lo, hi) for lo, hi in pieces]
         backs = [weigh_and_turn_back(bank, lo, hi) for bank, (lo, hi) in zip(turned, pieces)]
+        add_and_store(nc.vector, later_first[:, PLAIN:], last_second[:], PLAIN, TURNED_FROM)
         for (lo, hi), back in zip(pieces, backs):
             add_and_store(nc.vector, back[:], turned_second[:, lo - TURNED_FROM : hi - TURNED_FROM], lo, hi)
+        for lo, hi in spans(PLAIN_PIECES):
+            plain = keep.tile([P, hi - lo], F32, name="staged", bufs=len(TURNED_PIECES))
+            fetch_plain(plain, 1, lo, hi)
+            product = keep.tile([P, hi - lo], F32, name=f"product{lo}")
+            nc.vector.tensor_tensor(product[:], plain[:], gate_second[:, lo:hi], MULT)
+            add_and_store(nc.vector, product[:], later_first[:, lo:hi], lo, hi)

@@ -10,7 +10,7 @@ P = 128
 PACK = 4
 K_PASS = P * PACK
 PASSES = K // K_PASS
-WIDE = 2 * S
+HELD = 128
 BANK = 512
 
 FLOPS = 2 * K * N * S
@@ -32,8 +32,8 @@ SHARES = ((512, 256), (0, 384), (0, 0, 256))
 UNITS = ((256, 256, 512, 128, 128, 256), (512, 256, 256, 128, 128, 256), (512, 512, 128, 128, 256))
 BYTE_CUTS = (768, 512, 512, 256)
 WORD_CUTS = (768, 512, 256, 256, 128, 128)
-TURNED_PIECES = (256, 256, 256)
-PLAIN_PIECES = (256, 256, 128)
+TURNED_PIECES = (256, 256, 256, 128)
+PLAIN_PIECES = (256, 256)
 TURNED = sum(TURNED_PIECES)
 PLAIN = sum(PLAIN_PIECES)
 TURNED_FROM = T - TURNED
@@ -52,9 +52,7 @@ def tile_moe_cap2_lin_relu2_kernel(tc, xT, w_words, w_scales, b, gate, offs, pos
 
         offs_sb = keep.tile([P, S // 16], U16, name="offs_sb")
         pos_sb = [keep.tile([P, T // 16], U16, name=f"pos_sb{g}") for g in range(2)]
-        early_codes = keep.tile([P, T + WIDE], U32, name="early_codes", align_bytes=64)
-        last_codes = keep.tile([P, T], U32, name="last_codes", align_bytes=64)
-        codes = [early_codes[:, T:], early_codes[:], last_codes[:]]
+        codes = [keep.tile([P, T], U32, name=f"codes{a}", align_bytes=64) for a in range(PASSES)]
         planes = keep.tile([P, S], U8, name="planes", align_bytes=64)
         slot_codes = [keep.tile([P, S], U32, name=f"slot_codes{a}", align_bytes=64) for a in range(PASSES)]
         slot_planes = keep.tile([P, S], U8, name="slot_planes", align_bytes=64)
@@ -75,12 +73,11 @@ def tile_moe_cap2_lin_relu2_kernel(tc, xT, w_words, w_scales, b, gate, offs, pos
         nc.vector.memset(gate_rows[:], 0.0)
         nc.vector.memset(w_planes[:].bitcast(I32), 0)
         nc.vector.memset(planes[:].bitcast(I32), 0)
-        nc.vector.memset(early_codes[:, 2 * T :].bitcast(I32), 0)
 
         raws = {}
         for a in range(PASSES):
             for lo, hi in spans(LOADS[a]):
-                raw = keep.tile([P, PACK, hi - lo], F32, name=f"raw{a}_{lo}")
+                raw = keep.tile([P, PACK, hi - lo], F32, name=f"raw{a}_{lo}", align_bytes=64)
                 nc.sync.dma_start(out=raw[:], in_=xT[a * K_PASS : (a + 1) * K_PASS, lo:hi].rearrange("(p j) t -> p j t", j=PACK))
                 raws[a, lo] = raw
             if a == 0:
@@ -124,8 +121,14 @@ def tile_moe_cap2_lin_relu2_kernel(tc, xT, w_words, w_scales, b, gate, offs, pos
         def gather(dst, window, lo, hi):
             nc.vector.tensor_copy(dst[:, lo:hi], window.indirect(offs_sb[:, lo // 16 : hi // 16]))
 
+        held = []
         for a in range(PASSES - 1):
-            gather(slot_codes[a], codes[a][:, :WIDE], 0, S)
+            for lo, hi in spans(((S - HELD) // 2, (S - HELD) // 2)):
+                gather(slot_codes[a], codes[a][:], lo, hi)
+            last_load = spans(LOADS[a + 1])[-1][0]
+            late = keep.tile([P, HELD], U32, name=f"raw{a + 1}_{last_load}", align_bytes=64)
+            nc.vector.tensor_copy(late[:], codes[a][:].indirect(offs_sb[:, (S - HELD) // 16 :]))
+            held.append(late)
 
         gate_bank = psum.tile([P, P], F32, name="bank", bufs=8)
         nc.tensor.transpose(gate_bank[:], gate_rows[:], ident[:])
@@ -134,11 +137,12 @@ def tile_moe_cap2_lin_relu2_kernel(tc, xT, w_words, w_scales, b, gate, offs, pos
         def multiply(acc, first, width, a):
             e = first // C
             slots = slice(first, first + width)
+            words = held[a][:] if a < PASSES - 1 and first == S - HELD else slot_codes[a][:, slots]
             nc.tensor.matmul_mx(
                 out=acc[:],
                 lhsT=w_sb[:, e * PASSES + a, :].bitcast(FP8X4),
                 lhsT_scale=w_planes[:, e * PASSES + a, :],
-                rhs=slot_codes[a][:, slots].bitcast(FP8X4),
+                rhs=words.bitcast(FP8X4),
                 rhs_scale=slot_planes[4 * a : P, slots],
                 start=(a == 0),
                 stop=(a == PASSES - 1),
@@ -155,7 +159,7 @@ def tile_moe_cap2_lin_relu2_kernel(tc, xT, w_words, w_scales, b, gate, offs, pos
                         banks[first] = psum.tile([P, width], F32, name="bank", bufs=8)
                         for a in range(PASSES - 1):
                             multiply(banks[first], first, width, a)
-            gather(slot_codes[PASSES - 1], last_codes[:], lo, hi)
+            gather(slot_codes[PASSES - 1], codes[PASSES - 1][:], lo, hi)
             groups = [(first, width) for first, width in all_groups if lo <= first < hi]
             sums = [banks[first] for first, width in groups]
             for (first, width), acc in zip(groups, sums):

@@ -203,23 +203,26 @@ def tile_moe_cap2_lin_relu2_kernel(tc, xT, w_words, w_scales, b, gate, offs, pos
                 nc.tensor.transpose(back[:, c : c + P], by_token[:, c : c + P], ident[:])
             return back
 
-        def add_and_store(engine, first, second, lo, hi):
-            total = keep.tile([P, hi - lo], F32, name=f"total{lo}")
-            engine.tensor_tensor(total[:], first, second, ADD)
+        def add_and_store(tag, first, second, lo, hi):
+            total = keep.tile([P, hi - lo], F32, name=tag if tag == "y" else f"total{lo}")
+            nc.vector.tensor_tensor(total[:], first, second, ADD)
             nc.sync.dma_start(out=out[:, lo:hi], in_=total[:])
 
-        turned_second = fetch_weighed(1, TURNED_FROM, T, gate_second[:, TURNED_FROM:])
-        later_first = fetch_weighed(0, 0, TURNED_FROM, gate_first[:])
         last_second = fetch_weighed(1, PLAIN, TURNED_FROM, gate_second[:, PLAIN:TURNED_FROM])
+        later_first = fetch_weighed(0, 0, TURNED_FROM, gate_first[:])
+        turned_second = fetch_weighed(1, TURNED_FROM, T, gate_second[:, TURNED_FROM:])
         pieces = spans(TURNED_PIECES, TURNED_FROM)
         turned = [fetch_and_turn(lo, hi) for lo, hi in pieces]
         backs = [weigh_and_turn_back(bank, lo, hi) for bank, (lo, hi) in zip(turned, pieces)]
-        add_and_store(nc.vector, later_first[:, PLAIN:], last_second[:], PLAIN, TURNED_FROM)
+        add_and_store("total", later_first[:, PLAIN:], last_second[:], PLAIN, TURNED_FROM)
         for (lo, hi), back in zip(pieces, backs):
-            add_and_store(nc.vector, back[:], turned_second[:, lo - TURNED_FROM : hi - TURNED_FROM], lo, hi)
+            add_and_store("total", back[:], turned_second[:, lo - TURNED_FROM : hi - TURNED_FROM], lo, hi)
+        products = []
         for lo, hi in spans(PLAIN_PIECES):
             plain = keep.tile([P, hi - lo], F32, name="staged", bufs=len(TURNED_PIECES))
             fetch_plain(plain, 1, lo, hi)
             product = keep.tile([P, hi - lo], F32, name=f"product{lo}")
             nc.vector.tensor_tensor(product[:], plain[:], gate_second[:, lo:hi], MULT)
-            add_and_store(nc.vector, product[:], later_first[:, lo:hi], lo, hi)
+            products.append(product)
+        for (lo, hi), product, tag in zip(spans(PLAIN_PIECES), products, ("y", "total")):
+            add_and_store(tag, product[:], later_first[:, lo:hi], lo, hi)

@@ -32,10 +32,9 @@ SHARES = ((512, 256), (0, 384), (0, 0, 256))
 UNITS = ((256, 256, 512, 128, 128, 256), (512, 256, 256, 128, 128, 256), (512, 512, 128, 128, 256))
 BYTE_CUTS = (768, 512, 512, 256)
 WORD_CUTS = (768, 512, 256, 256, 128, 128)
-TURNED_PIECES = (256, 256, 256, 128)
-PLAIN_PIECES = (256, 256)
+TURNED_PIECES = (256, 256, 256, 256, 128)
+SECOND_CUT = 512
 TURNED = sum(TURNED_PIECES)
-PLAIN = sum(PLAIN_PIECES)
 TURNED_FROM = T - TURNED
 GATE_ROWS = TURNED // P
 
@@ -194,7 +193,7 @@ def tile_moe_cap2_lin_relu2_kernel(tc, xT, w_words, w_scales, b, gate, offs, pos
             return turned
 
         def weigh_and_turn_back(turned, lo, hi):
-            by_token = keep.tile([P, hi - lo], F32, name="staged", bufs=len(TURNED_PIECES))
+            by_token = keep.tile([P, hi - lo], F32, name=f"by_token{lo}")
             for c in range(0, hi - lo, P):
                 block = (lo - TURNED_FROM + c) // P
                 nc.scalar.activation(by_token[:, c : c + P], turned[:, c : c + P], ACT.Copy, scale=gate_cols[:, block : block + 1])
@@ -203,26 +202,20 @@ def tile_moe_cap2_lin_relu2_kernel(tc, xT, w_words, w_scales, b, gate, offs, pos
                 nc.tensor.transpose(back[:, c : c + P], by_token[:, c : c + P], ident[:])
             return back
 
-        def add_and_store(tag, first, second, lo, hi):
-            total = keep.tile([P, hi - lo], F32, name=tag if tag == "y" else f"total{lo}")
+        def add_and_store(first, second, lo, hi):
+            total = keep.tile([P, hi - lo], F32, name=f"total{lo}")
             nc.vector.tensor_tensor(total[:], first, second, ADD)
             nc.sync.dma_start(out=out[:, lo:hi], in_=total[:])
 
-        last_second = fetch_weighed(1, PLAIN, TURNED_FROM, gate_second[:, PLAIN:TURNED_FROM])
-        later_first = fetch_weighed(0, 0, TURNED_FROM, gate_first[:])
-        turned_second = fetch_weighed(1, TURNED_FROM, T, gate_second[:, TURNED_FROM:])
+        direct_second = fetch_weighed(1, 0, TURNED_FROM, gate_second[:, :TURNED_FROM])
+        direct_first = fetch_weighed(0, 0, TURNED_FROM, gate_first[:])
+        cut = TURNED_FROM + SECOND_CUT
+        early_second = fetch_weighed(1, TURNED_FROM, cut, gate_second[:, TURNED_FROM:cut])
+        add_and_store(direct_first[:], direct_second[:], 0, TURNED_FROM)
+        late_second = fetch_weighed(1, cut, T, gate_second[:, cut:])
         pieces = spans(TURNED_PIECES, TURNED_FROM)
         turned = [fetch_and_turn(lo, hi) for lo, hi in pieces]
-        backs = [weigh_and_turn_back(bank, lo, hi) for bank, (lo, hi) in zip(turned, pieces)]
-        add_and_store("total", later_first[:, PLAIN:], last_second[:], PLAIN, TURNED_FROM)
-        for (lo, hi), back in zip(pieces, backs):
-            add_and_store("total", back[:], turned_second[:, lo - TURNED_FROM : hi - TURNED_FROM], lo, hi)
-        products = []
-        for lo, hi in spans(PLAIN_PIECES):
-            plain = keep.tile([P, hi - lo], F32, name="staged", bufs=len(TURNED_PIECES))
-            fetch_plain(plain, 1, lo, hi)
-            product = keep.tile([P, hi - lo], F32, name=f"product{lo}")
-            nc.vector.tensor_tensor(product[:], plain[:], gate_second[:, lo:hi], MULT)
-            products.append(product)
-        for (lo, hi), product, tag in zip(spans(PLAIN_PIECES), products, ("y", "total")):
-            add_and_store(tag, product[:], later_first[:, lo:hi], lo, hi)
+        for bank, (lo, hi) in zip(turned, pieces):
+            back = weigh_and_turn_back(bank, lo, hi)
+            second = early_second[:, lo - TURNED_FROM : hi - TURNED_FROM] if lo < cut else late_second[:, lo - cut : hi - cut]
+            add_and_store(back[:], second, lo, hi)

@@ -29,7 +29,7 @@ MAX = mybir.AluOpType.max
 
 LOADS = ((1024, 512), (768, 768), (512, 512, 512))
 SHARES = ((512, 256), (0, 384), (0, 0, 256))
-UNITS = ((256, 256, 512, 128, 128, 256), (512, 256, 256, 128, 128, 256), (512, 512, 128, 128, 256))
+UNITS = ((256, 256, 256, 256, 128, 128, 128, 128), (512, 256, 256, 128, 256, 128), (512, 512, 128, 128, 128, 128))
 BYTE_CUTS = (768, 512, 512, 256)
 WORD_CUTS = (768, 512, 256, 256, 128, 128)
 TURNED_PIECES = (256, 256, 256, 256, 128)
@@ -97,25 +97,25 @@ def tile_moe_cap2_lin_relu2_kernel(tc, xT, w_words, w_scales, b, gate, offs, pos
         nc.sync.dma_start(out=gate_first[:], in_=gate[0, :, :TURNED_FROM])
 
         for a in range(PASSES):
-            for u0, u1 in spans(UNITS[a]):
-                grouped = keep.tile([P, u1 - u0, PACK], BF16, name=f"grouped{a}_{u0}", align_bytes=64)
-                for (l0, l1), share in zip(spans(LOADS[a]), SHARES[a]):
-                    for lo, hi, on_vector in ((l0, l1 - share, False), (l1 - share, l1, True)):
-                        lo, hi = max(lo, u0), min(hi, u1)
-                        if lo >= hi:
-                            continue
-                        run = 4 if on_vector else 2
-                        dst = grouped[:, lo - u0 : hi - u0, :].rearrange("p (c i) j -> p c j i", i=run)
-                        source = raws[a, l0][:, :, lo - l0 : hi - l0].rearrange("p j (c i) -> p c j i", i=run)
-                        if on_vector:
-                            nc.vector.tensor_copy(dst, source)
-                        else:
-                            nc.scalar.activation(dst, source, ACT.Copy)
-                nc.vector.quantize_mx(
-                    out=codes[a][:, u0:u1].bitcast(FP8X4),
-                    scales=planes[4 * a : P, u0:u1],
-                    in_=grouped[:].rearrange("p t j -> p (t j)"),
-                )
+            units = spans(UNITS[a])
+            grouped = {u0: keep.tile([P, u1 - u0, PACK], BF16, name=f"grouped{a}_{u0}", align_bytes=64) for u0, u1 in units}
+            for (l0, l1), share in zip(spans(LOADS[a]), SHARES[a]):
+                mine = [(u0, u1) for u0, u1 in units if l0 <= u0 < l1]
+                for u0, u1 in mine:
+                    on_vector = u0 >= l1 - share
+                    run = 4 if on_vector else 2
+                    dst = grouped[u0][:].rearrange("p (c i) j -> p c j i", i=run)
+                    source = raws[a, l0][:, :, u0 - l0 : u1 - l0].rearrange("p j (c i) -> p c j i", i=run)
+                    if on_vector:
+                        nc.vector.tensor_copy(dst, source)
+                    else:
+                        nc.scalar.activation(dst, source, ACT.Copy)
+                for u0, u1 in mine:
+                    nc.vector.quantize_mx(
+                        out=codes[a][:, u0:u1].bitcast(FP8X4),
+                        scales=planes[4 * a : P, u0:u1],
+                        in_=grouped[u0][:].rearrange("p t j -> p (t j)"),
+                    )
 
         def gather(dst, window, lo, hi):
             nc.vector.tensor_copy(dst[:, lo:hi], window.indirect(offs_sb[:, lo // 16 : hi // 16]))

@@ -11,7 +11,6 @@ PACK = 4
 K_PASS = P * PACK
 PASSES = K // K_PASS
 HELD = 128
-BANK = 512
 
 FLOPS = 2 * K * N * S
 
@@ -28,10 +27,16 @@ ADD = mybir.AluOpType.add
 MAX = mybir.AluOpType.max
 
 LOADS = ((1024, 512), (768, 768), (512, 512, 512))
-SHARES = ((512, 256), (0, 384), (0, 0, 256))
-UNITS = ((256, 256, 256, 256, 128, 128, 128, 128), (512, 256, 256, 128, 256, 128), (512, 512, 128, 128, 128, 128))
-BYTE_CUTS = (768, 512, 512, 256)
-WORD_CUTS = (768, 512, 256, 256, 128, 128)
+CALLS = (
+    ((("s", 256),), (("s", 256),), (("v", 256),), (("v", 256),), (("s", 128),), (("s", 128),), (("v", 128),), (("v", 128),)),
+    ((("s", 512),), (("s", 256),), (("s", 256),), (("s", 128),), (("v", 256),), (("v", 128),)),
+    ((("s", 512),), (("s", 512),), (("s", 128),), (("s", 128),), (("v", 128),), (("v", 128),)),
+)
+FIRST_ROW = (0, 4, 8)
+LATE_GATHERS = (
+    ("bytes", 768), ("words", 768), ("bytes", 512), ("words", 512), ("bytes", 512),
+    ("words", 256), ("bytes", 256), ("words", 256), ("words", 128), ("words", 128),
+)
 TURNED_PIECES = (256, 256, 256, 256, 128)
 SECOND_CUT = 512
 TURNED = sum(TURNED_PIECES)
@@ -73,9 +78,10 @@ def tile_moe_cap2_lin_relu2_kernel(tc, xT, w_words, w_scales, b, gate, offs, pos
         nc.vector.memset(w_planes[:].bitcast(I32), 0)
         nc.vector.memset(planes[:].bitcast(I32), 0)
 
+        load_spans = [spans(LOADS[a]) for a in range(PASSES)]
         raws = {}
         for a in range(PASSES):
-            for lo, hi in spans(LOADS[a]):
+            for lo, hi in load_spans[a]:
                 raw = keep.tile([P, PACK, hi - lo], F32, name=f"raw{a}_{lo}", align_bytes=64)
                 nc.sync.dma_start(out=raw[:], in_=xT[a * K_PASS : (a + 1) * K_PASS, lo:hi].rearrange("(p j) t -> p j t", j=PACK))
                 raws[a, lo] = raw
@@ -96,26 +102,30 @@ def tile_moe_cap2_lin_relu2_kernel(tc, xT, w_words, w_scales, b, gate, offs, pos
         nc.sync.dma_start(out=gate_second[:], in_=gate[1])
         nc.sync.dma_start(out=gate_first[:], in_=gate[0, :, :TURNED_FROM])
 
+        def round_tokens(on_vector, dst, source):
+            run = 4 if on_vector else 2
+            dst = dst.rearrange("p (c i) j -> p c j i", i=run)
+            source = source.rearrange("p j (c i) -> p c j i", i=run)
+            if on_vector:
+                nc.vector.tensor_copy(dst, source)
+            else:
+                nc.scalar.activation(dst, source, ACT.Copy)
+
         for a in range(PASSES):
-            units = spans(UNITS[a])
-            grouped = {u0: keep.tile([P, u1 - u0, PACK], BF16, name=f"grouped{a}_{u0}", align_bytes=64) for u0, u1 in units}
-            for (l0, l1), share in zip(spans(LOADS[a]), SHARES[a]):
-                mine = [(u0, u1) for u0, u1 in units if l0 <= u0 < l1]
-                for u0, u1 in mine:
-                    on_vector = u0 >= l1 - share
-                    run = 4 if on_vector else 2
-                    dst = grouped[u0][:].rearrange("p (c i) j -> p c j i", i=run)
-                    source = raws[a, l0][:, :, u0 - l0 : u1 - l0].rearrange("p j (c i) -> p c j i", i=run)
-                    if on_vector:
-                        nc.vector.tensor_copy(dst, source)
-                    else:
-                        nc.scalar.activation(dst, source, ACT.Copy)
-                for u0, u1 in mine:
-                    nc.vector.quantize_mx(
-                        out=codes[a][:, u0:u1].bitcast(FP8X4),
-                        scales=planes[4 * a : P, u0:u1],
-                        in_=grouped[u0][:].rearrange("p t j -> p (t j)"),
-                    )
+            call_spans = spans([sum(width for engine, width in call) for call in CALLS[a]])
+            grouped = [keep.tile([P, u1 - u0, PACK], BF16, name=f"grouped{a}_{u0}", align_bytes=64) for u0, u1 in call_spans]
+            for l0, l1 in load_spans[a]:
+                for (u0, u1), call, tile in zip(call_spans, CALLS[a], grouped):
+                    for (engine, width), (lo, hi) in zip(call, spans([width for engine, width in call], u0)):
+                        if l0 <= lo < l1:
+                            round_tokens(engine == "v", tile[:, lo - u0 : hi - u0, :], raws[a, l0][:, :, lo - l0 : hi - l0])
+                for (u0, u1), tile in zip(call_spans, grouped):
+                    if l0 < u1 <= l1:
+                        nc.vector.quantize_mx(
+                            out=codes[a][:, u0:u1].bitcast(FP8X4),
+                            scales=planes[FIRST_ROW[a] : P, u0:u1],
+                            in_=tile[:].rearrange("p t j -> p (t j)"),
+                        )
 
         def gather(dst, window, lo, hi):
             nc.vector.tensor_copy(dst[:, lo:hi], window.indirect(offs_sb[:, lo // 16 : hi // 16]))
@@ -124,7 +134,7 @@ def tile_moe_cap2_lin_relu2_kernel(tc, xT, w_words, w_scales, b, gate, offs, pos
         for a in range(PASSES - 1):
             for lo, hi in spans(((S - HELD) // 2, (S - HELD) // 2)):
                 gather(slot_codes[a], codes[a][:], lo, hi)
-            last_load = spans(LOADS[a + 1])[-1][0]
+            last_load = load_spans[a + 1][-1][0]
             late = keep.tile([P, HELD], U32, name=f"raw{a + 1}_{last_load}", align_bytes=64)
             nc.vector.tensor_copy(late[:], codes[a][:].indirect(offs_sb[:, (S - HELD) // 16 :]))
             held.append(late)
@@ -142,34 +152,40 @@ def tile_moe_cap2_lin_relu2_kernel(tc, xT, w_words, w_scales, b, gate, offs, pos
                 lhsT=w_sb[:, e * PASSES + a, :].bitcast(FP8X4),
                 lhsT_scale=w_planes[:, e * PASSES + a, :],
                 rhs=words.bitcast(FP8X4),
-                rhs_scale=slot_planes[4 * a : P, slots],
+                rhs_scale=slot_planes[FIRST_ROW[a] : P, slots],
                 start=(a == 0),
                 stop=(a == PASSES - 1),
             )
 
         all_groups = [(e * C, C) for e in range(E - 1)] + [(S - C, P), (S - P, P)]
         banks = {}
-        byte_cuts = dict(spans(BYTE_CUTS))
-        for lo, hi in spans(WORD_CUTS):
-            if lo in byte_cuts:
-                gather(slot_planes, planes[:], lo, byte_cuts[lo])
-                for first, width in all_groups:
-                    if lo <= first < byte_cuts[lo]:
-                        banks[first] = psum.tile([P, width], F32, name="bank", bufs=8)
-                        for a in range(PASSES - 1):
-                            multiply(banks[first], first, width, a)
-            gather(slot_codes[PASSES - 1], codes[PASSES - 1][:], lo, hi)
+        done = {"bytes": 0, "words": 0}
+        finished = 0
+        for sort, count in LATE_GATHERS:
+            lo, hi = done[sort], done[sort] + count
+            done[sort] = hi
             groups = [(first, width) for first, width in all_groups if lo <= first < hi]
-            sums = [banks[first] for first, width in groups]
-            for (first, width), acc in zip(groups, sums):
-                multiply(acc, first, width, PASSES - 1)
+            if sort == "bytes":
+                gather(slot_planes, planes[:], lo, hi)
+                for first, width in groups:
+                    banks[first] = psum.tile([P, width], F32, name="bank", bufs=8)
+                    for a in range(PASSES - 1):
+                        multiply(banks[first], first, width, a)
+                continue
+            gather(slot_codes[PASSES - 1], codes[PASSES - 1][:], lo, hi)
+            for first, width in groups:
+                multiply(banks[first], first, width, PASSES - 1)
+            if hi == S - C:
+                continue
+            groups = [(first, width) for first, width in all_groups if finished <= first < hi]
+            finished = hi
             relus = [keep.tile([P, width], F32, name=f"relu{first}") for first, width in groups]
-            for (first, width), acc, relu in zip(groups, sums, relus):
+            for (first, width), relu in zip(groups, relus):
                 e = first // C
                 if first < S - P:
-                    nc.scalar.activation(relu[:], acc[:], ACT.Relu, bias=b_sb[:, e : e + 1])
+                    nc.scalar.activation(relu[:], banks[first][:], ACT.Relu, bias=b_sb[:, e : e + 1])
                 else:
-                    nc.vector.tensor_scalar(relu[:], acc[:], b_sb[:, e : e + 1], 0.0, ADD, MAX)
+                    nc.vector.tensor_scalar(relu[:], banks[first][:], b_sb[:, e : e + 1], 0.0, ADD, MAX)
             for (first, width), relu in zip(groups, relus):
                 if first < S - P:
                     nc.scalar.activation(y[:, first : first + width], relu[:], ACT.Square)

@@ -99,8 +99,8 @@ def tile_moe_cap2_lin_relu2_kernel(tc, xT, w_words, w_scales, b, gate, offs, pos
             )
         nc.sync.dma_start(pos_sb[0][:], pos1)
         nc.sync.dma_start(pos_sb[1][:], pos2)
-        nc.sync.dma_start(out=gate_second[:], in_=gate[1])
         nc.sync.dma_start(out=gate_first[:], in_=gate[0, :, :TURNED_FROM])
+        nc.sync.dma_start(out=gate_second[:], in_=gate[1])
 
         def round_tokens(on_vector, dst, source):
             run = 4 if on_vector else 2
@@ -223,8 +223,8 @@ def tile_moe_cap2_lin_relu2_kernel(tc, xT, w_words, w_scales, b, gate, offs, pos
             nc.vector.tensor_tensor(total[:], first, second, ADD)
             nc.sync.dma_start(out=out[:, lo:hi], in_=total[:])
 
-        direct_second = fetch_weighed(1, 0, TURNED_FROM, gate_second[:, :TURNED_FROM])
         direct_first = fetch_weighed(0, 0, TURNED_FROM, gate_first[:])
+        direct_second = fetch_weighed(1, 0, TURNED_FROM, gate_second[:, :TURNED_FROM])
         cut = TURNED_FROM + SECOND_CUT
         early_second = fetch_weighed(1, TURNED_FROM, cut, gate_second[:, TURNED_FROM:cut])
         add_and_store(direct_first[:], direct_second[:], 0, TURNED_FROM)

from contextlib import ExitStack

import concourse.mybir as mybir
from concourse.masks import make_identity

K, T, E, C, N = 1536, 1536, 8, 256, 128
S = E * C
PAD = 32
P = 128
PACK = 4
K_PASS = P * PACK
PASSES = K // K_PASS
HELD = 128

FLOPS = 2 * K * N * S

F32 = mybir.dt.float32
BF16 = mybir.dt.bfloat16
I32 = mybir.dt.int32
U32 = mybir.dt.uint32
U16 = mybir.dt.uint16
U8 = mybir.dt.uint8
FP8X4 = mybir.dt.float8_e4m3fn_x4
ACT = mybir.ActivationFunctionType
MULT = mybir.AluOpType.mult
ADD = mybir.AluOpType.add
MAX = mybir.AluOpType.max

LOADS = ((1024, 512), (768, 768), (512, 512, 512))
CALLS = (
    ((("s", 256),), (("s", 256),), (("v", 256),), (("v", 256),), (("s", 128),), (("s", 128),), (("v", 128),), (("v", 128),)),
    ((("s", 512),), (("s", 256),), (("s", 256),), (("s", 128),), (("v", 256),), (("v", 128),)),
    ((("s", 512),), (("s", 512),), (("s", 128),), (("s", 128),), (("v", 128),), (("v", 128),)),
)
FIRST_ROW = (0, 4, 8)
LATE_GATHERS = (
    ("bytes", 768), ("words", 768), ("bytes", 512), ("words", 512), ("bytes", 512),
    ("words", 256), ("bytes", 256), ("words", 256), ("words", 128), ("words", 128),
)
TURNED_PIECES = (256, 256, 256, 256, 128)
SECOND_CUT = 512
TURNED = sum(TURNED_PIECES)
TURNED_FROM = T - TURNED
GATE_ROWS = TURNED // P


def spans(widths, first=0):
    return [(first + sum(widths[:i]), first + sum(widths[: i + 1])) for i in range(len(widths))]


def tile_moe_cap2_lin_relu2_kernel(tc, xT, w_words, w_scales, b, gate, offs, pos1, pos2, out):
    nc = tc.nc
    with ExitStack() as ctx:
        keep = ctx.enter_context(tc.tile_pool(name="keep", bufs=1))
        psum = ctx.enter_context(tc.psum_pool(name="psum", bufs=1))

        offs_sb = keep.tile([P, S // 16], U16, name="offs_sb")
        pos_sb = [keep.tile([P, T // 16], U16, name=f"pos_sb{g}") for g in range(2)]
        codes = [keep.tile([P, T], U32, name=f"codes{a}", align_bytes=64) for a in range(PASSES)]
        planes = keep.tile([P, S], U8, name="planes", align_bytes=64)
        slot_codes = [keep.tile([P, S], U32, name=f"slot_codes{a}", align_bytes=64) for a in range(PASSES)]
        slot_planes = keep.tile([P, S], U8, name="slot_planes", align_bytes=64)
        w_sb = keep.tile([P, E * PASSES, N], U32, name="w_sb", align_bytes=64)
        w_planes = keep.tile([P, E * PASSES, N], U8, name="w_planes", align_bytes=64)
        b_sb = keep.tile([P, E], F32, name="b_sb")
        gate_first = keep.tile([P, TURNED_FROM], F32, name="gate_first")
        gate_second = keep.tile([P, T], F32, name="gate_second")
        gate_rows = keep.tile([P, P], F32, name="gate_rows")
        gate_cols = keep.tile([P, GATE_ROWS], F32, name="gate_cols")
        y = keep.tile([P, S + PAD], F32, name="y")
        zeros = keep.tile([P, PAD], F32, name="zeros")
        ident = keep.tile([P, P], F32, name="ident")
        make_identity(nc, ident[:])

        nc.vector.memset(zeros[:], 0.0)
        nc.scalar.activation(y[:, S : S + PAD], zeros[:], ACT.Square)
        nc.vector.memset(gate_rows[:], 0.0)
        nc.vector.memset(w_planes[:].bitcast(I32), 0)
        nc.vector.memset(planes[:].bitcast(I32), 0)

        load_spans = [spans(LOADS[a]) for a in range(PASSES)]
        raws = {}
        for a in range(PASSES):
            for lo, hi in load_spans[a]:
                raw = keep.tile([P, PACK, hi - lo], F32, name=f"raw{a}_{lo}", align_bytes=64)
                nc.sync.dma_start(out=raw[:], in_=xT[a * K_PASS : (a + 1) * K_PASS, lo:hi].rearrange("(p j) t -> p j t", j=PACK))
                raws[a, lo] = raw
            if a == 0:
                nc.sync.dma_start(offs_sb[:], offs)
        nc.sync.dma_start(out=b_sb[:], in_=b)
        scale_rows = w_scales.rearrange("e a (q r) n -> r q (e a) n", r=4)
        for r in range(4):
            nc.sync.dma_start(out=w_planes[r:P:32].bitcast(I32), in_=scale_rows[r].bitcast(I32))
        nc.sync.dma_start(out=gate_rows[:GATE_ROWS, :], in_=gate[0, 0, TURNED_FROM:].rearrange("(c t) -> c t", t=P))
        for e in range(0, E, 2):
            nc.sync.dma_start(
                out=w_sb[:, e * PASSES : (e + 2) * PASSES, :].bitcast(I32),
                in_=w_words[e : e + 2].rearrange("e a p n r -> p (e a) (n r)").bitcast(I32),
            )
        nc.sync.dma_start(pos_sb[0][:], pos1)
        nc.sync.dma_start(pos_sb[1][:], pos2)
        nc.sync.dma_start(out=gate_first[:], in_=gate[0, :, :TURNED_FROM])
        nc.sync.dma_start(out=gate_second[:], in_=gate[1])

        def round_tokens(on_vector, dst, source):
            run = 4 if on_vector else 2
            dst = dst.rearrange("p (c i) j -> p c j i", i=run)
            source = source.rearrange("p j (c i) -> p c j i", i=run)
            if on_vector:
                nc.vector.tensor_copy(dst, source)
            else:
                nc.scalar.activation(dst, source, ACT.Copy)

        for a in range(PASSES):
            call_spans = spans([sum(width for engine, width in call) for call in CALLS[a]])
            grouped = [keep.tile([P, u1 - u0, PACK], BF16, name=f"grouped{a}_{u0}", align_bytes=64) for u0, u1 in call_spans]
            for l0, l1 in load_spans[a]:
                for (u0, u1), call, tile in zip(call_spans, CALLS[a], grouped):
                    for (engine, width), (lo, hi) in zip(call, spans([width for engine, width in call], u0)):
                        if l0 <= lo < l1:
                            round_tokens(engine == "v", tile[:, lo - u0 : hi - u0, :], raws[a, l0][:, :, lo - l0 : hi - l0])
                for (u0, u1), tile in zip(call_spans, grouped):
                    if l0 < u1 <= l1:
                        nc.vector.quantize_mx(
                            out=codes[a][:, u0:u1].bitcast(FP8X4),
                            scales=planes[FIRST_ROW[a] : P, u0:u1],
                            in_=tile[:].rearrange("p t j -> p (t j)"),
                        )

        def gather(dst, window, lo, hi):
            nc.vector.tensor_copy(dst[:, lo:hi], window.indirect(offs_sb[:, lo // 16 : hi // 16]))

        held = []
        for a in range(PASSES - 1):
            for lo, hi in spans(((S - HELD) // 2, (S - HELD) // 2)):
                gather(slot_codes[a], codes[a][:], lo, hi)
            last_load = load_spans[a + 1][-1][0]
            late = keep.tile([P, HELD], U32, name=f"raw{a + 1}_{last_load}", align_bytes=64)
            nc.vector.tensor_copy(late[:], codes[a][:].indirect(offs_sb[:, (S - HELD) // 16 :]))
            held.append(late)

        gate_bank = psum.tile([P, P], F32, name="bank", bufs=8)
        nc.tensor.transpose(gate_bank[:], gate_rows[:], ident[:])
        nc.scalar.activation(gate_cols[:], gate_bank[:, :GATE_ROWS], ACT.Copy)

        def multiply(acc, first, width, a):
            e = first // C
            slots = slice(first, first + width)
            words = held[a][:] if a < PASSES - 1 and first == S - HELD else slot_codes[a][:, slots]
            nc.tensor.matmul_mx(
                out=acc[:],
                lhsT=w_sb[:, e * PASSES + a, :].bitcast(FP8X4),
                lhsT_scale=w_planes[:, e * PASSES + a, :],
                rhs=words.bitcast(FP8X4),
                rhs_scale=slot_planes[FIRST_ROW[a] : P, slots],
                start=(a == 0),
                stop=(a == PASSES - 1),
            )

        all_groups = [(e * C, C) for e in range(E - 1)] + [(S - C, P), (S - P, P)]
        banks = {}
        done = {"bytes": 0, "words": 0}
        finished = 0
        for sort, count in LATE_GATHERS:
            lo, hi = done[sort], done[sort] + count
            done[sort] = hi
            groups = [(first, width) for first, width in all_groups if lo <= first < hi]
            if sort == "bytes":
                gather(slot_planes, planes[:], lo, hi)
                for first, width in groups:
                    banks[first] = psum.tile([P, width], F32, name="bank", bufs=8)
                    for a in range(PASSES - 1):
                        multiply(banks[first], first, width, a)
                continue
            gather(slot_codes[PASSES - 1], codes[PASSES - 1][:], lo, hi)
            for first, width in groups:
                multiply(banks[first], first, width, PASSES - 1)
            if hi == S - C:
                continue
            groups = [(first, width) for first, width in all_groups if finished <= first < hi]
            finished = hi
            relus = [keep.tile([P, width], F32, name=f"relu{first}") for first, width in groups]
            for (first, width), relu in zip(groups, relus):
                e = first // C
                if first < S - P:
                    nc.scalar.activation(relu[:], banks[first][:], ACT.Relu, bias=b_sb[:, e : e + 1])
                else:
                    nc.vector.tensor_scalar(relu[:], banks[first][:], b_sb[:, e : e + 1], 0.0, ADD, MAX)
            for (first, width), relu in zip(groups, relus):
                if first < S - P:
                    nc.scalar.activation(y[:, first : first + width], relu[:], ACT.Square)
                else:
                    nc.vector.tensor_tensor(y[:, first : first + width], relu[:], relu[:], MULT)

        def fetch_weighed(g, lo, hi, weights):
            z = keep.tile([P, hi - lo], F32, name=f"weighed{g}_{lo}")
            nc.vector.tensor_tensor(z[:], y[:].indirect(pos_sb[g][:, lo // 16 : hi // 16]), weights, MULT)
            return z

        def fetch_plain(z, g, lo, hi):
            nc.scalar.activation(z[:], y[:].indirect(pos_sb[g][:, lo // 16 : hi // 16]), ACT.Copy)

        def fetch_and_turn(lo, hi):
            plain = keep.tile([P, hi - lo], F32, name=f"plain{lo}")
            fetch_plain(plain, 0, lo, hi)
            turned = psum.tile([P, hi - lo], F32, name="bank", bufs=8)
            for c in range(0, hi - lo, P):
                nc.tensor.transpose(turned[:, c : c + P], plain[:, c : c + P], ident[:])
            return turned

        def weigh_and_turn_back(turned, lo, hi):
            by_token = keep.tile([P, hi - lo], F32, name=f"by_token{lo}")
            for c in range(0, hi - lo, P):
                block = (lo - TURNED_FROM + c) // P
                nc.scalar.activation(by_token[:, c : c + P], turned[:, c : c + P], ACT.Copy, scale=gate_cols[:, block : block + 1])
            back = psum.tile([P, hi - lo], F32, name="bank", bufs=8)
            for c in range(0, hi - lo, P):
                nc.tensor.transpose(back[:, c : c + P], by_token[:, c : c + P], ident[:])
            return back

        def add_and_store(first, second, lo, hi):
            total = keep.tile([P, hi - lo], F32, name=f"total{lo}")
            nc.vector.tensor_tensor(total[:], first, second, ADD)
            nc.sync.dma_start(out=out[:, lo:hi], in_=total[:])

        direct_first = fetch_weighed(0, 0, TURNED_FROM, gate_first[:])
        direct_second = fetch_weighed(1, 0, TURNED_FROM, gate_second[:, :TURNED_FROM])
        cut = TURNED_FROM + SECOND_CUT
        early_second = fetch_weighed(1, TURNED_FROM, cut, gate_second[:, TURNED_FROM:cut])
        add_and_store(direct_first[:], direct_second[:], 0, TURNED_FROM)
        late_second = fetch_weighed(1, cut, T, gate_second[:, cut:])
        pieces = spans(TURNED_PIECES, TURNED_FROM)
        turned = [fetch_and_turn(lo, hi) for lo, hi in pieces]
        for bank, (lo, hi) in zip(turned, pieces):
            back = weigh_and_turn_back(bank, lo, hi)
            second = early_second[:, lo - TURNED_FROM : hi - TURNED_FROM] if lo < cut else late_second[:, lo - cut : hi - cut]
            add_and_store(back[:], second, lo, hi)
